import numpy as np
import ml_dtypes


def mxq(x, axis, fmt="e4m3"):
    dtype, down = {"e4m3": (ml_dtypes.float8_e4m3fn, 7), "e5m2": (ml_dtypes.float8_e5m2, 14)}[fmt]
    v = np.moveaxis(np.asarray(x, np.float32).astype(ml_dtypes.bfloat16).astype(np.float64), axis, -1)
    blocks = v.reshape(v.shape[:-1] + (-1, 32))
    amax = np.abs(blocks).max(-1, keepdims=True)
    byte = np.maximum(np.where(amax > 0, np.frexp(amax)[1] - 1 + 127, 0) - down, 1)
    scale = np.exp2(byte - 127.0)
    codes = (blocks / scale).astype(np.float32).astype(dtype).astype(np.float64)
    return np.moveaxis((codes * scale).reshape(v.shape), -1, axis)


WIDE = False


def mx_kscale(k):
    if not WIDE:
        return np.ones(k)
    levels = np.array([10, -10, 5, -5, 0])
    if k % 512:
        return np.exp2(np.random.permutation(np.resize(levels, k // 32))).repeat(32)
    a = np.empty((k // 512, 16))
    for p in range(k // 512):
        a[p, :8] = np.random.permutation(np.resize(levels, 8))
        for g in range(8):
            far = levels[np.abs(levels - a[p, g]) >= 10]
            a[p, g + 8] = far[np.random.randint(len(far))]
    return np.exp2(a.ravel()).repeat(32)


def f64(x):
    return np.asarray(x).astype(np.float64)


def striped(idx):
    return np.tile(idx.reshape(-1, 16).T, (8, 1)).astype(np.uint16)


def unstriped(offs):
    return offs[:16].T.reshape(-1).astype(np.int64)


def pack_weight(w):
    k, n = w.shape
    w = f64(np.asarray(w, np.float32).astype(ml_dtypes.bfloat16)).reshape(k // 32, 32, n)
    amax = np.abs(w).max(1)
    byte = np.clip(np.where(amax > 0, np.frexp(amax)[1] - 1 + 127 - 7, 1), 1, 254)
    scaled = (w * np.exp2(127.0 - byte)[:, None, :]).reshape(k, n).astype(np.float32)
    words = np.ascontiguousarray(scaled.reshape(k // 512, 128, 4, n).transpose(0, 1, 3, 2)).astype(ml_dtypes.float8_e4m3fn).view(np.uint8)
    return words, np.ascontiguousarray(byte.astype(np.uint8).reshape(k // 512, 16, n))


def unpack_weight(words, scales):
    g, p, n, _ = words.shape
    vals = np.ascontiguousarray(words).view(ml_dtypes.float8_e4m3fn).astype(np.float64) * np.repeat(np.exp2(scales.astype(np.float64) - 127.0), 8, axis=1)[..., None]
    return vals.transpose(0, 1, 3, 2).reshape(g * 512, n)


E2M1 = np.array([0.0, 0.5, 1.0, 1.5, 2.0, 3.0, 4.0, 6.0, -0.0, -0.5, -1.0, -1.5, -2.0, -3.0, -4.0, -6.0])


def pack_fp4(w):
    k, n = w.shape
    w = f64(np.asarray(w, np.float32).astype(ml_dtypes.bfloat16)).reshape(k // 32, 32, n)
    amax = np.abs(w).max(1)
    mant, ex = np.frexp(amax / 6.0)
    byte = np.clip(np.where(amax > 0, np.where(mant > 0.5, ex, ex - 1) + 127, 1), 1, 254)
    scaled = (w * np.exp2(127.0 - byte)[:, None, :]).reshape(k, n).astype(np.float32)
    c = np.ascontiguousarray(scaled.reshape(k // 512, 128, 4, n).transpose(0, 1, 3, 2)).astype(ml_dtypes.float4_e2m1fn).view(np.uint8) & 0xF
    words = (c[..., 0::2] | (c[..., 1::2] << 4)).reshape(k // 512, 128, 2 * n)
    return np.ascontiguousarray(words), np.ascontiguousarray(byte.astype(np.uint8).reshape(k // 512, 16, n))


def unpack_fp4(words, scales):
    g, _, n = scales.shape
    words = np.ascontiguousarray(words).reshape(g, 128, n, 2)
    nib = np.empty((g, 128, n, 4), np.uint8)
    nib[..., 0::2] = words & 0xF
    nib[..., 1::2] = words >> 4
    vals = E2M1[nib] * np.repeat(np.exp2(scales.astype(np.float64) - 127.0), 8, axis=1)[..., None]
    return vals.transpose(0, 1, 3, 2).reshape(g * 512, n)


def silu(v):
    return v / (1.0 + np.exp(-np.maximum(v, -700.0)))


K, T, S, D, V, H, N = 1024, 2048, 1024, 2, 512, 512, 128
P = 2 ** 7


def setup_inputs():
    n = np.random.standard_normal
    s = mx_kscale(K)[:, None]
    u = mx_kscale(H)
    packed_xT = pack_weight(n((K, T)) * s)
    packed_w2 = pack_fp4(n((H, N)) / np.sqrt(H) / u[:, None])
    return {
        "x_words": packed_xT[0],
        "x_scales": packed_xT[1],
        "w1": (n((K, H)) / np.sqrt(K) / s * u).astype(np.float32),
        "w2_words": packed_w2[0],
        "w2_scales": packed_w2[1],
        "gate": (np.tile(np.random.uniform(0.2, 1.0, (D, 1, V)) / np.sqrt(D), (1, P, 1))).astype(np.float32),
        "offs": striped(np.random.permutation(T)[:S]),
        "cen": striped(np.random.permutation(S)[:V]),
        "pos1": striped(np.random.permutation(S)[:V]),
        "pos2": striped(np.random.permutation(S)[:V]),
    }


def reference(x_words, x_scales, w1, w2_words, w2_scales, gate, offs, cen, pos1, pos2):
    xq = unpack_weight(x_words, x_scales)[:, unstriped(offs)]
    h = silu(mxq(f64(w1), 0, "e4m3").T @ xq)
    z = h[:, unstriped(cen)] - (h[:, unstriped(pos1)] * f64(gate)[0, :1] + h[:, unstriped(pos2)] * f64(gate)[1, :1])
    return unpack_fp4(w2_words, w2_scales).T @ mxq(z, 0, "e4m3")

@@ -1,0 +1,231 @@
+from contextlib import ExitStack
+
+import concourse.mybir as mybir
+from concourse.masks import make_identity
+
+K, T, S, V, H, N = 1024, 2048, 1024, 512, 512, 128
+FLOPS = 2 * K * H * S + 2 * H * N * V
+
+F32 = mybir.dt.float32
+BF16 = mybir.dt.bfloat16
+I32 = mybir.dt.int32
+U32 = mybir.dt.uint32
+U16 = mybir.dt.uint16
+U8 = mybir.dt.uint8
+FP8X4 = mybir.dt.float8_e4m3fn_x4
+FP4X4 = mybir.dt.float4_e2m1fn_x4
+SILU = mybir.ActivationFunctionType.Silu
+MULT = mybir.AluOpType.mult
+SUBTRACT = mybir.AluOpType.subtract
+
+P = 128
+PACK = 4
+PASSES = K // (P * PACK)
+TILES = H // P
+BANK = 512
+GROUPS = ((0, 2), (2, 3), (3, 4))
+W1_CHUNKS = ((0, 1), (1, 2), (2, 4))
+
+
+def tile_picked_lapl_silu_p_kernel(
+    tc, x_words, x_scales, w1, w2_words, w2_scales, gate, offs, cen, pos1, pos2, out
+):
+    nc = tc.nc
+    with ExitStack() as ctx:
+        lists = ctx.enter_context(tc.tile_pool(name="lists", bufs=1))
+        keep = ctx.enter_context(tc.tile_pool(name="keep", bufs=1))
+        psum = ctx.enter_context(tc.psum_pool(name="psum", bufs=1))
+
+        x_plane = keep.tile([P, T], U8, name="x_plane", align_bytes=64)
+        nc.gpsimd.memset(x_plane[:].bitcast(I32), 0)
+        warm_in = keep.tile([P, 1], F32, name="warm_in")
+        warm_out = keep.tile([P, 1], F32, name="warm_out")
+        nc.gpsimd.memset(warm_in[:], 0.0)
+        nc.scalar.activation(warm_out[:], warm_in[:], SILU)
+        w2_plane = keep.tile([P, N], U8, name="w2_plane", align_bytes=64)
+        nc.gpsimd.memset(w2_plane[:].bitcast(I32), 0)
+
+        offs_sb = lists.tile([P, S // 16], U16, name="offs_sb")
+        nc.sync.dma_start(offs_sb[:], offs)
+        for q in range(4):
+            nc.sync.dma_start(
+                x_plane[32 * q : 32 * q + 4 * PASSES, :].bitcast(I32),
+                x_scales[:, 4 * q : 4 * q + 4, :].bitcast(I32),
+            )
+
+        def load_list(name, src):
+            lst = lists.tile([P, V // 16], U16, name=name)
+            nc.sync.dma_start(lst[:], src)
+            return lst
+
+        cen_sb = load_list("cen_sb", cen)
+        pos1_sb = load_list("pos1_sb", pos1)
+        w1_raw = {}
+
+        def load_w1(chunk, g):
+            t0, t1 = chunk
+            raw = keep.tile([P, PACK, (t1 - t0) * P], F32, name=f"w1_raw{t0}_{g}")
+            rows = w1[g * P * PACK : (g + 1) * P * PACK, t0 * P : t1 * P]
+            nc.sync.dma_start(raw[:], rows.rearrange("(p j) c -> p j c", j=PACK))
+            for t in range(t0, t1):
+                w1_raw[t, g] = raw[:, :, (t - t0) * P : (t - t0 + 1) * P]
+
+        x_table = []
+        for g in range(PASSES):
+            tbl = keep.tile([P, T], I32, name=f"x_table{g}", align_bytes=64)
+            nc.sync.dma_start(tbl[:], x_words[g].rearrange("p n t -> p (n t)").bitcast(I32))
+            x_table.append(tbl)
+            load_w1(W1_CHUNKS[0], g)
+        for g in range(PASSES):
+            load_w1(W1_CHUNKS[1], g)
+        pos2_sb = load_list("pos2_sb", pos2)
+        gate_sb = keep.tile([P, 2, V], F32, name="gate_sb")
+        nc.sync.dma_start(gate_sb[:], gate.rearrange("d p v -> p d v"))
+        for g in range(PASSES):
+            load_w1(W1_CHUNKS[2], g)
+        w2_codes = keep.tile([P, 2 * N], U8, name="w2_codes", align_bytes=64)
+        nc.sync.dma_start(w2_codes[:].bitcast(I32), w2_words[0].bitcast(I32))
+        for q in range(4):
+            nc.sync.dma_start(
+                w2_plane[32 * q : 32 * q + 4, :].bitcast(I32),
+                w2_scales[0, 4 * q : 4 * q + 4, :].bitcast(I32),
+            )
+
+        identity = keep.tile([P, P], F32, name="identity")
+        make_identity(nc, identity[:])
+
+        picked_plane = keep.tile([P, S], U8, name="picked_plane", align_bytes=64)
+        nc.vector.tensor_copy(picked_plane[:], x_plane[:].indirect(offs_sb[:]))
+        picked = {}
+
+        def pick(g, half):
+            tag = "shared0_1" if (g, half) == (1, 1) else f"picked{g}_{half}"
+            words = keep.tile([P, BANK], U32, name=f"picked{g}_{half}", tag=tag, align_bytes=64)
+            cols = offs_sb[:, half * BANK // 16 : (half + 1) * BANK // 16]
+            nc.vector.tensor_copy(words[:], x_table[g][:].bitcast(U32).indirect(cols))
+            picked[g, half] = words
+
+        w1_q = {}
+
+        def round_w1(t, g, engine_copy):
+            grouped = keep.tile([P, P, PACK], BF16, name=f"w1_grouped{t}_{g}", tag=f"shared{t}_{g}", align_bytes=64)
+            engine_copy(grouped[:], w1_raw[t, g].rearrange("p j c -> p c j"))
+            return grouped
+
+        def quantize_w1(t, g, grouped):
+            codes = keep.tile([P, P], U32, name=f"w1_codes{t}_{g}", align_bytes=64)
+            plane = keep.tile([P, P], U8, name=f"w1_plane{t}_{g}", align_bytes=64)
+            nc.vector.quantize_mx(
+                out=codes[:].bitcast(FP8X4),
+                scales=plane[:],
+                in_=grouped[:].rearrange("p c j -> p (c j)"),
+            )
+            w1_q[t, g] = (codes, plane)
+
+        h = [keep.tile([P, S], F32, name=f"h{t}") for t in range(TILES)]
+
+        def first_layer(t, half):
+            cols = slice(half * BANK, (half + 1) * BANK)
+            acc = psum.tile([P, BANK], F32, name="h_acc", tag="wide_acc", bufs=4)
+            for g in range(PASSES):
+                codes, plane = w1_q[t, g]
+                nc.tensor.matmul_mx(
+                    out=acc[:],
+                    lhsT=codes[:].bitcast(FP8X4),
+                    lhsT_scale=plane[:],
+                    rhs=picked[g, half][:].bitcast(FP8X4),
+                    rhs_scale=picked_plane[4 * g : P, cols],
+                    start=(g == 0),
+                    stop=(g == PASSES - 1),
+                )
+            nc.scalar.activation(h[t][:, cols], acc[:], SILU)
+
+        pick(0, 0)
+        pick(0, 1)
+        quantize_w1(0, 0, round_w1(0, 0, nc.scalar.copy))
+        pick(1, 0)
+        quantize_w1(0, 1, round_w1(0, 1, nc.scalar.copy))
+        pick(1, 1)
+        quantize_w1(1, 0, round_w1(1, 0, nc.scalar.copy))
+        quantize_w1(1, 1, round_w1(1, 1, nc.vector.tensor_copy))
+        for half in range(2):
+            first_layer(0, half)
+        neg_gate = keep.tile([P, V], F32, name="neg_gate")
+        nc.vector.tensor_scalar_mul(neg_gate[:], gate_sb[:, 1, :], -1.0)
+
+        z_rows = [
+            keep.tile([P, b1 - b0, 2, P, 2], BF16, name=f"z_rows{b0}", align_bytes=64) for b0, b1 in GROUPS
+        ]
+
+        def laplacian(t, b0, b1):
+            width = (b1 - b0) * P
+            cols = slice(b0 * P, b1 * P)
+            entries = slice(b0 * P // 16, b1 * P // 16)
+            made = []
+            for d in range(3):
+                tag = f"shared{t + 1}_{d}" if d < PASSES and t + 1 < TILES else f"term{t}_{b0}_{d}"
+                made.append(keep.tile([P, width], F32, name=f"term{t}_{b0}_{d}", tag=tag, align_bytes=64))
+            first, second, own = made
+            nc.vector.tensor_tensor(first[:], h[t][:].indirect(pos1_sb[:, entries]), gate_sb[:, 0, cols], MULT)
+            nc.vector.tensor_tensor(second[:], h[t][:].indirect(pos2_sb[:, entries]), neg_gate[:, cols], MULT)
+            nc.vector.tensor_tensor(own[:], h[t][:].indirect(cen_sb[:, entries]), first[:], SUBTRACT)
+            terms = (second, own)
+            acc = psum.tile([P, 4, P], F32, name="z_acc", bufs=2)
+            for b in range(b1 - b0):
+                for d, term in enumerate(terms):
+                    nc.tensor.matmul(
+                        acc[:, b, :],
+                        lhsT=term[:, b * P : (b + 1) * P],
+                        rhs=identity[:],
+                        is_transpose=True,
+                        start=(d == 0),
+                        stop=(d == len(terms) - 1),
+                    )
+            for rows, (g0, g1) in zip(z_rows, GROUPS):
+                if g0 >= b0 and g1 <= b1:
+                    nc.scalar.copy(
+                        rows[:, :, :, 32 * t : 32 * (t + 1), :],
+                        acc[:, g0 - b0 : g1 - b0, :].rearrange("v b (p u e) -> v b u p e", u=2, e=2),
+                    )
+
+        def second_layer(rows, b0, b1):
+            nb = b1 - b0
+            width = nb * P
+            words = rows[:].rearrange("v b u p e -> v (b u p e)").bitcast(F32)
+            turned = psum.tile([P, 2, 2, P], F32, name="turned", bufs=2)
+            for b in range(nb):
+                for u in range(2):
+                    c0 = (2 * b + u) * P
+                    nc.tensor.transpose(turned[:, b, u, :], words[:, c0 : c0 + P], identity[:])
+            grouped = keep.tile([P, width * PACK], BF16, name=f"z_grouped{b0}", align_bytes=64)
+            nc.scalar.copy(
+                grouped[:].bitcast(F32).rearrange("p (b v u) -> p b v u", b=nb, u=2),
+                turned[:, 0:nb].rearrange("p b u v -> p b v u"),
+            )
+            codes = keep.tile([P, width], U32, name=f"z_codes{b0}", align_bytes=64)
+            plane = keep.tile([P, width], U8, name=f"z_plane{b0}", align_bytes=64)
+            nc.vector.quantize_mx(out=codes[:].bitcast(FP8X4), scales=plane[:], in_=grouped[:])
+            acc = psum.tile([P, BANK], F32, name="out_acc", tag="wide_acc", bufs=4)
+            nc.tensor.matmul_mx(
+                out=acc[:, 0:width],
+                lhsT=w2_codes[:].bitcast(FP4X4),
+                lhsT_scale=w2_plane[:],
+                rhs=codes[:].bitcast(FP8X4),
+                rhs_scale=plane[:],
+                start=True,
+                stop=True,
+            )
+            result = keep.tile([P, width], F32, name=f"result{b0}")
+            nc.scalar.copy(result[:], acc[:, 0:width])
+            nc.sync.dma_start(out[:, b0 * P : b1 * P], result[:])
+
+        for t in range(TILES - 1):
+            if t > 0:
+                for g in range(PASSES):
+                    quantize_w1(t + 1, g, round_w1(t + 1, g, nc.scalar.copy))
+            for half in range(2):
+                first_layer(t + 1, half)
+            laplacian(t, 0, 4)
+        for rows, (b0, b1) in zip(z_rows, GROUPS):
+            laplacian(TILES - 1, b0, b1)
+            second_layer(rows, b0, b1)

@@ -14,17 +14,22 @@ U16 = mybir.dt.uint16
 U8 = mybir.dt.uint8
 FP8X4 = mybir.dt.float8_e4m3fn_x4
 FP4X4 = mybir.dt.float4_e2m1fn_x4
+COPY = mybir.ActivationFunctionType.Copy
 SILU = mybir.ActivationFunctionType.Silu
 MULT = mybir.AluOpType.mult
 SUBTRACT = mybir.AluOpType.subtract
 
 P = 128
 PACK = 4
+QUADRANTS = 4
+PER_COLUMN = 16
 PASSES = K // (P * PACK)
-TILES = H // P
 BANK = 512
+BLOCKS = V // P
+NEIGHBOURS = 2
+
+W1_LOADS = ((0, 1), (1, 2), (2, 4))
 GROUPS = ((0, 2), (2, 3), (3, 4))
-W1_CHUNKS = ((0, 1), (1, 2), (2, 4))
 
 
 def tile_picked_lapl_silu_p_kernel(
@@ -36,56 +41,62 @@ def tile_picked_lapl_silu_p_kernel(
         keep = ctx.enter_context(tc.tile_pool(name="keep", bufs=1))
         psum = ctx.enter_context(tc.psum_pool(name="psum", bufs=1))
 
+        def bank(number, shape, name):
+            return psum.tile(shape, F32, name=name, tag=f"bank{number}")
+
         x_plane = keep.tile([P, T], U8, name="x_plane", align_bytes=64)
         nc.gpsimd.memset(x_plane[:].bitcast(I32), 0)
-        warm_in = keep.tile([P, 1], F32, name="warm_in")
-        warm_out = keep.tile([P, 1], F32, name="warm_out")
-        nc.gpsimd.memset(warm_in[:], 0.0)
-        nc.scalar.activation(warm_out[:], warm_in[:], SILU)
+        gate_rows = keep.tile([P, P], F32, name="gate_rows")
+        nc.gpsimd.memset(gate_rows[:], 0.0)
         w2_plane = keep.tile([P, N], U8, name="w2_plane", align_bytes=64)
         nc.gpsimd.memset(w2_plane[:].bitcast(I32), 0)
 
-        offs_sb = lists.tile([P, S // 16], U16, name="offs_sb")
-        nc.sync.dma_start(offs_sb[:], offs)
-        for q in range(4):
-            nc.sync.dma_start(
-                x_plane[32 * q : 32 * q + 4 * PASSES, :].bitcast(I32),
-                x_scales[:, 4 * q : 4 * q + 4, :].bitcast(I32),
-            )
+        def load_list(name, source, entries):
+            tile = lists.tile([P, entries // PER_COLUMN], U16, name=name)
+            nc.sync.dma_start(tile[:], source)
+            return tile
 
-        def load_list(name, src):
-            lst = lists.tile([P, V // 16], U16, name=name)
-            nc.sync.dma_start(lst[:], src)
-            return lst
-
-        cen_sb = load_list("cen_sb", cen)
-        pos1_sb = load_list("pos1_sb", pos1)
         w1_raw = {}
 
-        def load_w1(chunk, g):
-            t0, t1 = chunk
-            raw = keep.tile([P, PACK, (t1 - t0) * P], F32, name=f"w1_raw{t0}_{g}")
+        def load_w1(tiles, g):
+            t0, t1 = tiles
+            name = f"w1_raw{t0}_{g}"
+            raw = keep.tile([P, PACK, (t1 - t0) * P], F32, name=name, tag=name)
             rows = w1[g * P * PACK : (g + 1) * P * PACK, t0 * P : t1 * P]
             nc.sync.dma_start(raw[:], rows.rearrange("(p j) c -> p j c", j=PACK))
             for t in range(t0, t1):
                 w1_raw[t, g] = raw[:, :, (t - t0) * P : (t - t0 + 1) * P]
 
         x_table = []
+
+        def load_x(g):
+            table = keep.tile([P, T], I32, name=f"x_table{g}", align_bytes=64)
+            nc.sync.dma_start(table[:], x_words[g].rearrange("p n t -> p (n t)").bitcast(I32))
+            x_table.append(table)
+
+        offs_sb = load_list("offs_sb", offs, S)
+        for q in range(QUADRANTS):
+            nc.sync.dma_start(
+                x_plane[32 * q : 32 * q + 4 * PASSES, :].bitcast(I32),
+                x_scales[:, 4 * q : 4 * q + 4, :].bitcast(I32),
+            )
+        cen_sb = load_list("cen_sb", cen, V)
+        pos1_sb = load_list("pos1_sb", pos1, V)
+        load_x(0)
+        nc.sync.dma_start(
+            gate_rows[0 : NEIGHBOURS * BLOCKS, :], gate[:, 0, :].rearrange("d (b k) -> d b k", k=P)
+        )
+        load_w1(W1_LOADS[0], 0)
+        load_x(1)
+        load_w1(W1_LOADS[0], 1)
         for g in range(PASSES):
-            tbl = keep.tile([P, T], I32, name=f"x_table{g}", align_bytes=64)
-            nc.sync.dma_start(tbl[:], x_words[g].rearrange("p n t -> p (n t)").bitcast(I32))
-            x_table.append(tbl)
-            load_w1(W1_CHUNKS[0], g)
+            load_w1(W1_LOADS[1], g)
+        pos2_sb = load_list("pos2_sb", pos2, V)
         for g in range(PASSES):
-            load_w1(W1_CHUNKS[1], g)
-        pos2_sb = load_list("pos2_sb", pos2)
-        gate_sb = keep.tile([P, 2, V], F32, name="gate_sb")
-        nc.sync.dma_start(gate_sb[:], gate.rearrange("d p v -> p d v"))
-        for g in range(PASSES):
-            load_w1(W1_CHUNKS[2], g)
+            load_w1(W1_LOADS[2], g)
         w2_codes = keep.tile([P, 2 * N], U8, name="w2_codes", align_bytes=64)
         nc.sync.dma_start(w2_codes[:].bitcast(I32), w2_words[0].bitcast(I32))
-        for q in range(4):
+        for q in range(QUADRANTS):
             nc.sync.dma_start(
                 w2_plane[32 * q : 32 * q + 4, :].bitcast(I32),
                 w2_scales[0, 4 * q : 4 * q + 4, :].bitcast(I32),
@@ -96,116 +107,129 @@ def tile_picked_lapl_silu_p_kernel(
 
         picked_plane = keep.tile([P, S], U8, name="picked_plane", align_bytes=64)
         nc.vector.tensor_copy(picked_plane[:], x_plane[:].indirect(offs_sb[:]))
+
+        gate_turned = bank(2, [P, P], "gate_turned")
+        nc.tensor.transpose(gate_turned[:], gate_rows[:], identity[:])
+        gate_cols = keep.tile([P, NEIGHBOURS * BLOCKS], F32, name="gate_cols")
+        nc.scalar.copy(gate_cols[:], gate_turned[:, 0 : NEIGHBOURS * BLOCKS])
+        edge_weights = []
+        for d, sign in enumerate((1.0, -1.0)):
+            spread = bank(3 + d, [P, BLOCKS, P], "spread")
+            for b in range(BLOCKS):
+                column = gate_cols[:, BLOCKS * d + b : BLOCKS * d + b + 1]
+                nc.tensor.transpose(spread[:, b, :], column.to_broadcast([P, P]), identity[:])
+            signed = keep.tile([P, V], F32, name=f"edge_weights{d}")
+            nc.scalar.activation(signed[:], spread[:].rearrange("p b k -> p (b k)"), COPY, scale=sign)
+            edge_weights.append(signed)
+
         picked = {}
 
-        def pick(g, half):
-            tag = "shared0_1" if (g, half) == (1, 1) else f"picked{g}_{half}"
+        def pick(g, half, pieces, tag):
             words = keep.tile([P, BANK], U32, name=f"picked{g}_{half}", tag=tag, align_bytes=64)
-            cols = offs_sb[:, half * BANK // 16 : (half + 1) * BANK // 16]
-            nc.vector.tensor_copy(words[:], x_table[g][:].bitcast(U32).indirect(cols))
+            n = BANK // pieces
+            for i in range(pieces):
+                entry = half * BANK + i * n
+                offsets = offs_sb[:, entry // PER_COLUMN : (entry + n) // PER_COLUMN]
+                nc.vector.tensor_copy(words[:, i * n : (i + 1) * n], x_table[g][:].bitcast(U32).indirect(offsets))
             picked[g, half] = words
 
-        w1_q = {}
+        w1_mx = {}
 
-        def round_w1(t, g, engine_copy):
-            grouped = keep.tile([P, P, PACK], BF16, name=f"w1_grouped{t}_{g}", tag=f"shared{t}_{g}", align_bytes=64)
-            engine_copy(grouped[:], w1_raw[t, g].rearrange("p j c -> p c j"))
-            return grouped
-
-        def quantize_w1(t, g, grouped):
-            codes = keep.tile([P, P], U32, name=f"w1_codes{t}_{g}", align_bytes=64)
-            plane = keep.tile([P, P], U8, name=f"w1_plane{t}_{g}", align_bytes=64)
+        def quantize_w1(t, passes, copy):
+            n = len(passes)
+            name = f"w1_grouped{t}_{passes[0]}"
+            grouped = keep.tile([P, n, P, PACK], BF16, name=name, tag=name, align_bytes=64)
+            for i, g in enumerate(passes):
+                copy(grouped[:, i], w1_raw[t, g].rearrange("p j c -> p c j"))
+            codes = keep.tile([P, n * P], U32, name=f"w1_codes{t}_{passes[0]}", align_bytes=64)
+            plane = keep.tile([P, n * P], U8, name=f"w1_plane{t}_{passes[0]}", align_bytes=64)
             nc.vector.quantize_mx(
                 out=codes[:].bitcast(FP8X4),
                 scales=plane[:],
-                in_=grouped[:].rearrange("p c j -> p (c j)"),
+                in_=grouped[:].rearrange("p g c j -> p (g c j)"),
             )
-            w1_q[t, g] = (codes, plane)
+            for i, g in enumerate(passes):
+                w1_mx[t, g] = (codes[:, i * P : (i + 1) * P], plane[:, i * P : (i + 1) * P])
 
-        h = [keep.tile([P, S], F32, name=f"h{t}") for t in range(TILES)]
+        h = {}
 
-        def first_layer(t, half):
-            cols = slice(half * BANK, (half + 1) * BANK)
-            acc = psum.tile([P, BANK], F32, name="h_acc", tag="wide_acc", bufs=4)
-            for g in range(PASSES):
-                codes, plane = w1_q[t, g]
-                nc.tensor.matmul_mx(
-                    out=acc[:],
-                    lhsT=codes[:].bitcast(FP8X4),
-                    lhsT_scale=plane[:],
-                    rhs=picked[g, half][:].bitcast(FP8X4),
-                    rhs_scale=picked_plane[4 * g : P, cols],
-                    start=(g == 0),
-                    stop=(g == PASSES - 1),
-                )
-            nc.scalar.activation(h[t][:, cols], acc[:], SILU)
+        def first_layer(t, stretches, tag):
+            h[t] = keep.tile([P, S], F32, name=f"h{t}", tag=tag)
+            for c0, c1, number in stretches:
+                half = c0 // BANK
+                acc = bank(number, [P, c1 - c0], "h_acc")
+                for g in range(PASSES):
+                    codes, plane = w1_mx[t, g]
+                    nc.tensor.matmul_mx(
+                        out=acc[:],
+                        lhsT=codes.bitcast(FP8X4),
+                        lhsT_scale=plane,
+                        rhs=picked[g, half][:, c0 - half * BANK : c1 - half * BANK].bitcast(FP8X4),
+                        rhs_scale=picked_plane[4 * g : P, c0:c1],
+                        start=(g == 0),
+                        stop=(g == PASSES - 1),
+                    )
+                nc.scalar.activation(h[t][:, c0:c1], acc[:], SILU)
 
-        pick(0, 0)
-        pick(0, 1)
-        quantize_w1(0, 0, round_w1(0, 0, nc.scalar.copy))
-        pick(1, 0)
-        quantize_w1(0, 1, round_w1(0, 1, nc.scalar.copy))
-        pick(1, 1)
-        quantize_w1(1, 0, round_w1(1, 0, nc.scalar.copy))
-        quantize_w1(1, 1, round_w1(1, 1, nc.vector.tensor_copy))
-        for half in range(2):
-            first_layer(0, half)
-        neg_gate = keep.tile([P, V], F32, name="neg_gate")
-        nc.vector.tensor_scalar_mul(neg_gate[:], gate_sb[:, 1, :], -1.0)
+        pick(0, 0, 1, "picked0_0")
+        pick(0, 1, 1, "picked0_1")
+        quantize_w1(0, (0,), nc.scalar.copy)
+        pick(1, 0, 1, "picked1_0")
+        quantize_w1(0, (1,), nc.scalar.copy)
+        pick(1, 1, 2, "w1_grouped0_1")
+        quantize_w1(1, (0,), nc.scalar.copy)
+        quantize_w1(1, (1,), nc.vector.tensor_copy)
+        first_layer(0, ((0, 512, 0), (512, 768, 1), (768, 1024, 7)), "h0")
 
         z_rows = [
             keep.tile([P, b1 - b0, 2, P, 2], BF16, name=f"z_rows{b0}", align_bytes=64) for b0, b1 in GROUPS
         ]
 
-        def laplacian(t, b0, b1):
-            width = (b1 - b0) * P
-            cols = slice(b0 * P, b1 * P)
-            entries = slice(b0 * P // 16, b1 * P // 16)
-            made = []
-            for d in range(3):
-                tag = f"shared{t + 1}_{d}" if d < PASSES and t + 1 < TILES else f"term{t}_{b0}_{d}"
-                made.append(keep.tile([P, width], F32, name=f"term{t}_{b0}_{d}", tag=tag, align_bytes=64))
-            first, second, own = made
-            nc.vector.tensor_tensor(first[:], h[t][:].indirect(pos1_sb[:, entries]), gate_sb[:, 0, cols], MULT)
-            nc.vector.tensor_tensor(second[:], h[t][:].indirect(pos2_sb[:, entries]), neg_gate[:, cols], MULT)
-            nc.vector.tensor_tensor(own[:], h[t][:].indirect(cen_sb[:, entries]), first[:], SUBTRACT)
-            terms = (second, own)
-            acc = psum.tile([P, 4, P], F32, name="z_acc", bufs=2)
+        def laplacian(t, b0, b1, number, copy):
+            targets = slice(b0 * P, b1 * P)
+            columns = slice(b0 * P // PER_COLUMN, b1 * P // PER_COLUMN)
+            first, second, own = [
+                keep.tile([P, (b1 - b0) * P], F32, name=f"{name}{t}_{b0}") for name in ("first", "second", "own")
+            ]
+            nc.vector.tensor_tensor(first[:], h[t][:].indirect(pos1_sb[:, columns]), edge_weights[0][:, targets], MULT)
+            nc.vector.tensor_tensor(second[:], h[t][:].indirect(pos2_sb[:, columns]), edge_weights[1][:, targets], MULT)
+            nc.vector.tensor_tensor(own[:], h[t][:].indirect(cen_sb[:, columns]), first[:], SUBTRACT)
+            acc = bank(number, [P, b1 - b0, P], "z_acc")
             for b in range(b1 - b0):
-                for d, term in enumerate(terms):
+                for term, opens in ((second, True), (own, False)):
                     nc.tensor.matmul(
                         acc[:, b, :],
                         lhsT=term[:, b * P : (b + 1) * P],
                         rhs=identity[:],
                         is_transpose=True,
-                        start=(d == 0),
-                        stop=(d == len(terms) - 1),
+                        start=opens,
+                        stop=not opens,
                     )
             for rows, (g0, g1) in zip(z_rows, GROUPS):
                 if g0 >= b0 and g1 <= b1:
-                    nc.scalar.copy(
+                    copy(
                         rows[:, :, :, 32 * t : 32 * (t + 1), :],
                         acc[:, g0 - b0 : g1 - b0, :].rearrange("v b (p u e) -> v b u p e", u=2, e=2),
                     )
 
-        def second_layer(rows, b0, b1):
-            nb = b1 - b0
-            width = nb * P
-            words = rows[:].rearrange("v b u p e -> v (b u p e)").bitcast(F32)
-            turned = psum.tile([P, 2, 2, P], F32, name="turned", bufs=2)
-            for b in range(nb):
+        def second_layer(group, turn_banks, out_bank, copy):
+            b0, b1 = GROUPS[group]
+            width = (b1 - b0) * P
+            pairs = z_rows[group][:].rearrange("v b u p e -> v (b u p e)").bitcast(F32)
+            grouped = keep.tile([P, width * PACK], BF16, name=f"z_grouped{b0}", align_bytes=64)
+            for b in range(b1 - b0):
+                turned = bank(turn_banks[b], [P, 2, P], "turned")
                 for u in range(2):
                     c0 = (2 * b + u) * P
-                    nc.tensor.transpose(turned[:, b, u, :], words[:, c0 : c0 + P], identity[:])
-            grouped = keep.tile([P, width * PACK], BF16, name=f"z_grouped{b0}", align_bytes=64)
-            nc.scalar.copy(
-                grouped[:].bitcast(F32).rearrange("p (b v u) -> p b v u", b=nb, u=2),
-                turned[:, 0:nb].rearrange("p b u v -> p b v u"),
-            )
+                    nc.tensor.transpose(turned[:, u, :], pairs[:, c0 : c0 + P], identity[:])
+                nc.scalar.copy(
+                    grouped[:, b * P * PACK : (b + 1) * P * PACK].bitcast(F32).rearrange("p (v u) -> p v u", u=2),
+                    turned[:].rearrange("p u v -> p v u"),
+                )
             codes = keep.tile([P, width], U32, name=f"z_codes{b0}", align_bytes=64)
             plane = keep.tile([P, width], U8, name=f"z_plane{b0}", align_bytes=64)
             nc.vector.quantize_mx(out=codes[:].bitcast(FP8X4), scales=plane[:], in_=grouped[:])
-            acc = psum.tile([P, BANK], F32, name="out_acc", tag="wide_acc", bufs=4)
+            acc = bank(out_bank, [P, BANK], "out_acc")
             nc.tensor.matmul_mx(
                 out=acc[:, 0:width],
                 lhsT=w2_codes[:].bitcast(FP4X4),
@@ -216,16 +240,22 @@ def tile_picked_lapl_silu_p_kernel(
                 stop=True,
             )
             result = keep.tile([P, width], F32, name=f"result{b0}")
-            nc.scalar.copy(result[:], acc[:, 0:width])
+            copy(result[:], acc[:, 0:width])
             nc.sync.dma_start(out[:, b0 * P : b1 * P], result[:])
 
-        for t in range(TILES - 1):
-            if t > 0:
-                for g in range(PASSES):
-                    quantize_w1(t + 1, g, round_w1(t + 1, g, nc.scalar.copy))
-            for half in range(2):
-                first_layer(t + 1, half)
-            laplacian(t, 0, 4)
-        for rows, (b0, b1) in zip(z_rows, GROUPS):
-            laplacian(TILES - 1, b0, b1)
-            second_layer(rows, b0, b1)
+        quantize_w1(2, (0, 1), nc.scalar.copy)
+        quantize_w1(3, (0, 1), nc.scalar.copy)
+        first_layer(1, ((0, 512, 2), (512, 1024, 3)), "w1_raw2_1")
+        first_layer(2, ((0, 512, 0), (512, 1024, 1)), "h2")
+        first_layer(3, ((0, 512, 2), (512, 1024, 3)), "h3")
+
+        laplacian(0, 0, BLOCKS, 1, nc.scalar.copy)
+        laplacian(1, 0, BLOCKS, 3, nc.scalar.copy)
+        laplacian(2, 0, 3, 4, nc.scalar.copy)
+        laplacian(3, 0, 2, 5, nc.scalar.copy)
+        second_layer(0, (6, 7), 3, nc.scalar.copy)
+        laplacian(2, 3, 4, 2, nc.scalar.copy)
+        laplacian(3, 2, 3, 6, nc.scalar.copy)
+        second_layer(1, (0,), 4, nc.scalar.copy)
+        laplacian(3, 3, 4, 7, nc.vector.tensor_copy)
+        second_layer(2, (1,), 5, nc.vector.tensor_copy)

@@ -48,6 +48,10 @@ def tile_picked_lapl_silu_p_kernel(
         nc.gpsimd.memset(x_plane[:].bitcast(I32), 0)
         gate_rows = keep.tile([P, P], F32, name="gate_rows")
         nc.gpsimd.memset(gate_rows[:], 0.0)
+        warm_in = keep.tile([P, 1], F32, name="warm_in")
+        warm_out = keep.tile([P, 1], F32, name="warm_out")
+        nc.gpsimd.memset(warm_in[:], 0.0)
+        nc.scalar.activation(warm_out[:], warm_in[:], SILU)
         w2_plane = keep.tile([P, N], U8, name="w2_plane", align_bytes=64)
         nc.gpsimd.memset(w2_plane[:].bitcast(I32), 0)
 
@@ -81,11 +85,11 @@ def tile_picked_lapl_silu_p_kernel(
                 x_scales[:, 4 * q : 4 * q + 4, :].bitcast(I32),
             )
         cen_sb = load_list("cen_sb", cen, V)
-        pos1_sb = load_list("pos1_sb", pos1, V)
-        load_x(0)
         nc.sync.dma_start(
             gate_rows[0 : NEIGHBOURS * BLOCKS, :], gate[:, 0, :].rearrange("d (b k) -> d b k", k=P)
         )
+        load_x(0)
+        pos1_sb = load_list("pos1_sb", pos1, V)
         load_w1(W1_LOADS[0], 0)
         load_x(1)
         load_w1(W1_LOADS[0], 1)

@@ -144,7 +144,10 @@ def tile_picked_lapl_silu_p_kernel(
             name = f"w1_grouped{t}_{passes[0]}"
             grouped = keep.tile([P, n, P, PACK], BF16, name=name, tag=name, align_bytes=64)
             for i, g in enumerate(passes):
-                copy(grouped[:, i], w1_raw[t, g].rearrange("p j c -> p c j"))
+                copy(
+                    grouped[:, i].rearrange("p (c i) j -> p c j i", i=PACK),
+                    w1_raw[t, g].rearrange("p j (c i) -> p c j i", i=PACK),
+                )
             codes = keep.tile([P, n * P], U32, name=f"w1_codes{t}_{passes[0]}", align_bytes=64)
             plane = keep.tile([P, n * P], U8, name=f"w1_plane{t}_{passes[0]}", align_bytes=64)
             nc.vector.quantize_mx(

@@ -17,7 +17,6 @@ FP4X4 = mybir.dt.float4_e2m1fn_x4
 COPY = mybir.ActivationFunctionType.Copy
 SILU = mybir.ActivationFunctionType.Silu
 MULT = mybir.AluOpType.mult
-SUBTRACT = mybir.AluOpType.subtract
 
 P = 128
 PACK = 4
@@ -29,7 +28,6 @@ BLOCKS = V // P
 NEIGHBOURS = 2
 
 W1_LOADS = ((0, 1), (1, 2), (2, 4))
-GROUPS = ((0, 2), (2, 3), (3, 4))
 
 
 def tile_picked_lapl_silu_p_kernel(
@@ -39,6 +37,7 @@ def tile_picked_lapl_silu_p_kernel(
     with ExitStack() as ctx:
         lists = ctx.enter_context(tc.tile_pool(name="lists", bufs=1))
         keep = ctx.enter_context(tc.tile_pool(name="keep", bufs=1))
+        placed = ctx.enter_context(tc.tile_pool(name="placed", bufs=1))
         psum = ctx.enter_context(tc.psum_pool(name="psum", bufs=1))
 
         def bank(number, shape, name):
@@ -64,12 +63,11 @@ def tile_picked_lapl_silu_p_kernel(
 
         def load_w1(tiles, g):
             t0, t1 = tiles
-            name = f"w1_raw{t0}_{g}"
-            raw = keep.tile([P, PACK, (t1 - t0) * P], F32, name=name, tag=name)
+            raw = keep.tile([P, PACK, (t1 - t0) * P], F32, name=f"w1_raw{t0}_{g}")
             rows = w1[g * P * PACK : (g + 1) * P * PACK, t0 * P : t1 * P]
             nc.sync.dma_start(raw[:], rows.rearrange("(p j) c -> p j c", j=PACK))
             for t in range(t0, t1):
-                w1_raw[t, g] = raw[:, :, (t - t0) * P : (t - t0 + 1) * P]
+                w1_raw[t, g] = (raw, t0)
 
         x_table = []
 
@@ -116,52 +114,64 @@ def tile_picked_lapl_silu_p_kernel(
         nc.tensor.transpose(gate_turned[:], gate_rows[:], identity[:])
         gate_cols = keep.tile([P, NEIGHBOURS * BLOCKS], F32, name="gate_cols")
         nc.scalar.copy(gate_cols[:], gate_turned[:, 0 : NEIGHBOURS * BLOCKS])
-        edge_weights = []
-        for d, sign in enumerate((1.0, -1.0)):
+        edge_weights = {}
+        for d in range(NEIGHBOURS):
             spread = bank(3 + d, [P, BLOCKS, P], "spread")
             for b in range(BLOCKS):
                 column = gate_cols[:, BLOCKS * d + b : BLOCKS * d + b + 1]
                 nc.tensor.transpose(spread[:, b, :], column.to_broadcast([P, P]), identity[:])
             signed = keep.tile([P, V], F32, name=f"edge_weights{d}")
-            nc.scalar.activation(signed[:], spread[:].rearrange("p b k -> p (b k)"), COPY, scale=sign)
-            edge_weights.append(signed)
+            nc.scalar.activation(signed[:], spread[:].rearrange("p b k -> p (b k)"), COPY, scale=-1.0)
+            edge_weights[d, "all"] = signed
+            early = keep.tile([P, V // 2], F32, name=f"early_weights{d}", tag=f"early_weights{d}")
+            nc.scalar.activation(early[:], spread[:, 0:2, :].rearrange("p b k -> p (b k)"), COPY, scale=-1.0)
+            edge_weights[d, "early"] = early
 
         picked = {}
 
-        def pick(g, half, pieces, tag):
-            words = keep.tile([P, BANK], U32, name=f"picked{g}_{half}", tag=tag, align_bytes=64)
-            n = BANK // pieces
+        def pick(g, e0, e1, pieces, tag):
+            words = keep.tile([P, e1 - e0], U32, name=f"picked{g}_{e0}", tag=tag, align_bytes=64)
+            n = (e1 - e0) // pieces
             for i in range(pieces):
-                entry = half * BANK + i * n
+                entry = e0 + i * n
                 offsets = offs_sb[:, entry // PER_COLUMN : (entry + n) // PER_COLUMN]
                 nc.vector.tensor_copy(words[:, i * n : (i + 1) * n], x_table[g][:].bitcast(U32).indirect(offsets))
-            picked[g, half] = words
+            for half in range(e0 // BANK, e1 // BANK):
+                picked[g, half] = words[:, half * BANK - e0 : (half + 1) * BANK - e0]
 
+        w1_grouped = {}
         w1_mx = {}
 
-        def quantize_w1(t, passes, copy):
-            n = len(passes)
-            name = f"w1_grouped{t}_{passes[0]}"
-            grouped = keep.tile([P, n, P, PACK], BF16, name=name, tag=name, align_bytes=64)
-            for i, g in enumerate(passes):
-                copy(
-                    grouped[:, i].rearrange("p (c i) j -> p c j i", i=PACK),
-                    w1_raw[t, g].rearrange("p j (c i) -> p c j i", i=PACK),
-                )
-            codes = keep.tile([P, n * P], U32, name=f"w1_codes{t}_{passes[0]}", align_bytes=64)
-            plane = keep.tile([P, n * P], U8, name=f"w1_plane{t}_{passes[0]}", align_bytes=64)
-            nc.vector.quantize_mx(
-                out=codes[:].bitcast(FP8X4),
-                scales=plane[:],
-                in_=grouped[:].rearrange("p g c j -> p (g c j)"),
+        def rounded_tile(name, parts, offset=None):
+            shape = [P, len(parts) * P * PACK]
+            if offset is None:
+                tile = keep.tile(shape, BF16, name=name, tag=name, align_bytes=64)
+            else:
+                tile = placed.tile(shape, BF16, name=name, offset=offset, align_bytes=64)
+            w1_grouped[name] = (tile, parts)
+
+        def round_w1(name, t0, t1, g, copy):
+            tile, parts = w1_grouped[name]
+            first = parts.index((t0, g))
+            raw, base = w1_raw[t0, g]
+            copy(
+                tile[:, first * P * PACK : (first + t1 - t0) * P * PACK].rearrange("p (c i j) -> p c j i", i=PACK, j=PACK),
+                raw[:, :, (t0 - base) * P : (t1 - base) * P].rearrange("p j (c i) -> p c j i", i=PACK),
             )
-            for i, g in enumerate(passes):
-                w1_mx[t, g] = (codes[:, i * P : (i + 1) * P], plane[:, i * P : (i + 1) * P])
+
+        def quantize_w1(name, tag=None):
+            tile, parts = w1_grouped[name]
+            width = len(parts) * P
+            codes = keep.tile([P, width], U32, name=f"{name}_codes", tag=tag or f"{name}_codes", align_bytes=64)
+            plane = keep.tile([P, width], U8, name=f"{name}_plane", align_bytes=64)
+            nc.vector.quantize_mx(out=codes[:].bitcast(FP8X4), scales=plane[:], in_=tile[:])
+            for i, part in enumerate(parts):
+                w1_mx[part] = (codes[:, i * P : (i + 1) * P], plane[:, i * P : (i + 1) * P])
 
         h = {}
 
-        def first_layer(t, stretches, tag):
-            h[t] = keep.tile([P, S], F32, name=f"h{t}", tag=tag)
+        def first_layer(t, stretches):
+            h[t] = keep.tile([P, S], F32, name=f"h{t}")
             for c0, c1, number in stretches:
                 half = c0 // BANK
                 acc = bank(number, [P, c1 - c0], "h_acc")
@@ -178,67 +188,100 @@ def tile_picked_lapl_silu_p_kernel(
                     )
                 nc.scalar.activation(h[t][:, c0:c1], acc[:], SILU)
 
-        pick(0, 0, 1, "picked0_0")
-        pick(0, 1, 1, "picked0_1")
-        quantize_w1(0, (0,), nc.scalar.copy)
-        pick(1, 0, 1, "picked1_0")
-        quantize_w1(0, (1,), nc.scalar.copy)
-        pick(1, 1, 2, "w1_grouped0_1")
-        quantize_w1(1, (0,), nc.scalar.copy)
-        quantize_w1(1, (1,), nc.vector.tensor_copy)
-        first_layer(0, ((0, 512, 0), (512, 768, 1), (768, 1024, 7)), "h0")
+        rounded_tile("w1_00", [(0, 0)])
+        rounded_tile("w1_01", [(0, 1)])
+        rounded_tile("w1_1", [(1, 0), (1, 1)])
+        rounded_tile("w1_23", [(2, 0), (3, 0), (2, 1), (3, 1)], 2048)
+        round_w1("w1_00", 0, 1, 0, nc.scalar.copy)
+        round_w1("w1_01", 0, 1, 1, nc.scalar.copy)
+        round_w1("w1_1", 1, 2, 0, nc.scalar.copy)
+        round_w1("w1_1", 1, 2, 1, nc.scalar.copy)
+        pick(0, 0, S, 1, "picked0")
+        quantize_w1("w1_00")
+        pick(1, 0, BANK, 1, "picked1_0")
+        quantize_w1("w1_01")
+        pick(1, BANK, S, 2, "w1_01")
+        first_layer(0, ((0, 512, 0), (512, 768, 1), (768, 1024, 7)))
+        quantize_w1("w1_1")
+        round_w1("w1_23", 2, 4, 0, nc.vector.tensor_copy)
+        round_w1("w1_23", 2, 4, 1, nc.vector.tensor_copy)
+        quantize_w1("w1_23")
 
-        z_rows = [
-            keep.tile([P, b1 - b0, 2, P, 2], BF16, name=f"z_rows{b0}", align_bytes=64) for b0, b1 in GROUPS
-        ]
+        z_rows = keep.tile([P, BLOCKS * H], BF16, name="z_rows", align_bytes=64)
+        z_view = z_rows[:].rearrange("v (b u p e) -> v b u p e", b=BLOCKS, u=2, e=2)
+        z_pairs = z_rows[:].bitcast(F32)
 
-        def laplacian(t, b0, b1, number, copy):
-            targets = slice(b0 * P, b1 * P)
+        terms = {}
+        sums = {}
+
+        def keep_terms(name, t, b0, b1, tile):
+            for b in range(b0, b1):
+                terms[name, t, b] = tile[:, (b - b0) * P : (b - b0 + 1) * P]
+
+        def centres(t, b0, b1):
+            own = keep.tile([P, (b1 - b0) * P], F32, name=f"own{t}_{b0}", tag=f"own{t}")
             columns = slice(b0 * P // PER_COLUMN, b1 * P // PER_COLUMN)
-            first, second, own = [
-                keep.tile([P, (b1 - b0) * P], F32, name=f"{name}{t}_{b0}") for name in ("first", "second", "own")
-            ]
-            nc.vector.tensor_tensor(first[:], h[t][:].indirect(pos1_sb[:, columns]), edge_weights[0][:, targets], MULT)
-            nc.vector.tensor_tensor(second[:], h[t][:].indirect(pos2_sb[:, columns]), edge_weights[1][:, targets], MULT)
-            nc.vector.tensor_tensor(own[:], h[t][:].indirect(cen_sb[:, columns]), first[:], SUBTRACT)
+            nc.scalar.activation(own[:], h[t][:].indirect(cen_sb[:, columns]), COPY)
+            keep_terms("own", t, b0, b1, own)
+
+        def neighbours(d, t, b0, b1, term=None, weights="all"):
+            if term is None:
+                term = keep.tile([P, (b1 - b0) * P], F32, name=f"neighbour{d}_{t}_{b0}")
+            columns = slice(b0 * P // PER_COLUMN, b1 * P // PER_COLUMN)
+            offsets = (pos1_sb, pos2_sb)[d][:, columns]
+            nc.vector.tensor_tensor(term[:], h[t][:].indirect(offsets), edge_weights[d, weights][:, b0 * P : b1 * P], MULT)
+            keep_terms(d, t, b0, b1, term)
+
+        def add_terms(t, b0, b1, number):
             acc = bank(number, [P, b1 - b0, P], "z_acc")
-            for b in range(b1 - b0):
-                for term, opens in ((second, True), (own, False)):
+            for b in range(b0, b1):
+                for i, name in enumerate(("own", 0, 1)):
                     nc.tensor.matmul(
-                        acc[:, b, :],
-                        lhsT=term[:, b * P : (b + 1) * P],
+                        acc[:, b - b0, :],
+                        lhsT=terms[name, t, b],
                         rhs=identity[:],
                         is_transpose=True,
-                        start=opens,
-                        stop=not opens,
+                        start=(i == 0),
+                        stop=(i == 2),
                     )
-            for rows, (g0, g1) in zip(z_rows, GROUPS):
-                if g0 >= b0 and g1 <= b1:
-                    copy(
-                        rows[:, :, :, 32 * t : 32 * (t + 1), :],
-                        acc[:, g0 - b0 : g1 - b0, :].rearrange("v b (p u e) -> v b u p e", u=2, e=2),
-                    )
+            sums[t, b0] = acc
 
-        def second_layer(group, turn_banks, out_bank, copy):
-            b0, b1 = GROUPS[group]
-            width = (b1 - b0) * P
-            pairs = z_rows[group][:].rearrange("v b u p e -> v (b u p e)").bitcast(F32)
-            grouped = keep.tile([P, width * PACK], BF16, name=f"z_grouped{b0}", align_bytes=64)
-            for b in range(b1 - b0):
-                turned = bank(turn_banks[b], [P, 2, P], "turned")
+        def round_z(t, start, b0, b1, copy):
+            copy(
+                z_view[:, b0:b1, :, 32 * t : 32 * (t + 1), :],
+                sums[t, start][:, b0 - start : b1 - start, :].rearrange("v b (p u e) -> v b u p e", u=2, e=2),
+            )
+
+        z_grouped = {}
+
+        def turn_back(b0, b1, numbers, copy):
+            grouped = keep.tile([P, (b1 - b0) * P * PACK], BF16, name=f"z_grouped{b0}", align_bytes=64)
+            for b in range(b0, b1):
+                turned = bank(numbers[b - b0], [P, 2, P], "turned")
                 for u in range(2):
                     c0 = (2 * b + u) * P
-                    nc.tensor.transpose(turned[:, u, :], pairs[:, c0 : c0 + P], identity[:])
-                nc.scalar.copy(
-                    grouped[:, b * P * PACK : (b + 1) * P * PACK].bitcast(F32).rearrange("p (v u) -> p v u", u=2),
+                    nc.tensor.transpose(turned[:, u, :], z_pairs[:, c0 : c0 + P], identity[:])
+                copy(
+                    grouped[:, (b - b0) * P * PACK : (b - b0 + 1) * P * PACK].bitcast(F32).rearrange("p (v u) -> p v u", u=2),
                     turned[:].rearrange("p u v -> p v u"),
                 )
+            z_grouped[b0] = grouped
+
+        z_mx = {}
+
+        def quantize_z(b0, b1):
+            width = (b1 - b0) * P
             codes = keep.tile([P, width], U32, name=f"z_codes{b0}", align_bytes=64)
             plane = keep.tile([P, width], U8, name=f"z_plane{b0}", align_bytes=64)
-            nc.vector.quantize_mx(out=codes[:].bitcast(FP8X4), scales=plane[:], in_=grouped[:])
-            acc = bank(out_bank, [P, BANK], "out_acc")
+            nc.vector.quantize_mx(out=codes[:].bitcast(FP8X4), scales=plane[:], in_=z_grouped[b0][:])
+            z_mx[b0] = (codes, plane)
+
+        def second_layer(b0, b1, number, copy):
+            width = (b1 - b0) * P
+            codes, plane = z_mx[b0]
+            acc = bank(number, [P, width], "out_acc")
             nc.tensor.matmul_mx(
-                out=acc[:, 0:width],
+                out=acc[:],
                 lhsT=w2_codes[:].bitcast(FP4X4),
                 lhsT_scale=w2_plane[:],
                 rhs=codes[:].bitcast(FP8X4),
@@ -247,22 +290,55 @@ def tile_picked_lapl_silu_p_kernel(
                 stop=True,
             )
             result = keep.tile([P, width], F32, name=f"result{b0}")
-            copy(result[:], acc[:, 0:width])
+            copy(result[:], acc[:])
             nc.sync.dma_start(out[:, b0 * P : b1 * P], result[:])
 
-        quantize_w1(2, (0, 1), nc.scalar.copy)
-        quantize_w1(3, (0, 1), nc.scalar.copy)
-        first_layer(1, ((0, 512, 2), (512, 1024, 3)), "w1_raw2_1")
-        first_layer(2, ((0, 512, 0), (512, 1024, 1)), "h2")
-        first_layer(3, ((0, 512, 2), (512, 1024, 3)), "h3")
-
-        laplacian(0, 0, BLOCKS, 1, nc.scalar.copy)
-        laplacian(1, 0, BLOCKS, 3, nc.scalar.copy)
-        laplacian(2, 0, 3, 4, nc.scalar.copy)
-        laplacian(3, 0, 2, 5, nc.scalar.copy)
-        second_layer(0, (6, 7), 3, nc.scalar.copy)
-        laplacian(2, 3, 4, 2, nc.scalar.copy)
-        laplacian(3, 2, 3, 6, nc.scalar.copy)
-        second_layer(1, (0,), 4, nc.scalar.copy)
-        laplacian(3, 3, 4, 7, nc.vector.tensor_copy)
-        second_layer(2, (1,), 5, nc.vector.tensor_copy)
+        on_scalar, on_vector = nc.scalar.copy, nc.vector.tensor_copy
+        first_layer(1, ((0, 512, 2), (512, 1024, 3)))
+        centres(0, 0, 4)
+        first_layer(2, ((0, 512, 4), (512, 1024, 5)))
+        first_layer(3, ((0, 512, 0), (512, 1024, 1)))
+        both0 = placed.tile([P, 2 * V], F32, name="both0", offset=0)
+        both1 = placed.tile([P, 2 * V], F32, name="both1", offset=4096)
+        neighbours(0, 0, 0, 4, both0[:, 0:V])
+        neighbours(1, 0, 0, 4, both0[:, V : 2 * V])
+        neighbours(0, 1, 0, 4, both1[:, 0:V])
+        neighbours(1, 1, 0, 4, both1[:, V : 2 * V])
+        add_terms(0, 0, 4, 4)
+        centres(1, 0, 4)
+        centres(2, 0, 4)
+        add_terms(1, 0, 4, 5)
+        centres(3, 0, 2)
+        round_z(0, 0, 0, 4, on_scalar)
+        round_z(1, 0, 0, 4, on_scalar)
+        neighbours(0, 2, 0, 2)
+        neighbours(1, 2, 0, 2)
+        add_terms(2, 0, 2, 6)
+        neighbours(0, 3, 0, 2, None, "early")
+        neighbours(1, 3, 0, 2, None, "early")
+        add_terms(3, 0, 2, 7)
+        round_z(2, 0, 0, 2, on_scalar)
+        round_z(3, 0, 0, 2, on_scalar)
+        centres(3, 2, 4)
+        for d in range(NEIGHBOURS):
+            late = keep.tile([P, V // 2], F32, name=f"late{d}", tag=f"early_weights{d}")
+            neighbours(d, 2, 2, 4, late)
+        add_terms(2, 2, 4, 0)
+        round_z(2, 2, 2, 4, on_scalar)
+        turn_back(0, 2, (2, 3), on_scalar)
+        neighbours(0, 3, 2, 3)
+        neighbours(1, 3, 2, 3)
+        add_terms(3, 2, 3, 1)
+        neighbours(0, 3, 3, 4)
+        neighbours(1, 3, 3, 4)
+        add_terms(3, 3, 4, 4)
+        round_z(3, 2, 2, 3, on_scalar)
+        round_z(3, 3, 3, 4, on_vector)
+        quantize_z(0, 2)
+        turn_back(2, 3, (5,), on_scalar)
+        turn_back(3, 4, (6,), on_vector)
+        second_layer(0, 2, 7, on_scalar)
+        quantize_z(2, 3)
+        quantize_z(3, 4)
+        second_layer(2, 3, 0, on_scalar)
+        second_layer(3, 4, 2, on_vector)

@@ -127,17 +127,13 @@ def tile_picked_lapl_silu_p_kernel(
             nc.scalar.activation(early[:], spread[:, 0:2, :].rearrange("p b k -> p (b k)"), COPY, scale=-1.0)
             edge_weights[d, "early"] = early
 
-        picked = {}
+        picked = {0: [], 1: []}
 
-        def pick(g, e0, e1, pieces, tag):
+        def pick(g, e0, e1, tag):
             words = keep.tile([P, e1 - e0], U32, name=f"picked{g}_{e0}", tag=tag, align_bytes=64)
-            n = (e1 - e0) // pieces
-            for i in range(pieces):
-                entry = e0 + i * n
-                offsets = offs_sb[:, entry // PER_COLUMN : (entry + n) // PER_COLUMN]
-                nc.vector.tensor_copy(words[:, i * n : (i + 1) * n], x_table[g][:].bitcast(U32).indirect(offsets))
-            for half in range(e0 // BANK, e1 // BANK):
-                picked[g, half] = words[:, half * BANK - e0 : (half + 1) * BANK - e0]
+            offsets = offs_sb[:, e0 // PER_COLUMN : e1 // PER_COLUMN]
+            nc.vector.tensor_copy(words[:], x_table[g][:].bitcast(U32).indirect(offsets))
+            picked[g].append((e0, e1, words))
 
         w1_grouped = {}
         w1_mx = {}
@@ -170,23 +166,28 @@ def tile_picked_lapl_silu_p_kernel(
 
         h = {}
 
-        def first_layer(t, stretches):
-            h[t] = keep.tile([P, S], F32, name=f"h{t}")
-            for c0, c1, number in stretches:
-                half = c0 // BANK
-                acc = bank(number, [P, c1 - c0], "h_acc")
-                for g in range(PASSES):
-                    codes, plane = w1_mx[t, g]
-                    nc.tensor.matmul_mx(
-                        out=acc[:],
-                        lhsT=codes.bitcast(FP8X4),
-                        lhsT_scale=plane,
-                        rhs=picked[g, half][:, c0 - half * BANK : c1 - half * BANK].bitcast(FP8X4),
-                        rhs_scale=picked_plane[4 * g : P, c0:c1],
-                        start=(g == 0),
-                        stop=(g == PASSES - 1),
-                    )
-                nc.scalar.activation(h[t][:, c0:c1], acc[:], SILU)
+        def first_layer(t, c0, c1, number):
+            if t not in h:
+                h[t] = keep.tile([P, S], F32, name=f"h{t}")
+            acc = bank(number, [P, c1 - c0], "h_acc")
+            runs = [
+                (g, max(c0, e0), min(c1, e1), e0, words)
+                for g in range(PASSES)
+                for e0, e1, words in picked[g]
+                if e0 < c1 and e1 > c0
+            ]
+            for i, (g, a, b, e0, words) in enumerate(runs):
+                codes, plane = w1_mx[t, g]
+                nc.tensor.matmul_mx(
+                    out=acc[:, a - c0 : b - c0],
+                    lhsT=codes.bitcast(FP8X4),
+                    lhsT_scale=plane,
+                    rhs=words[:, a - e0 : b - e0].bitcast(FP8X4),
+                    rhs_scale=picked_plane[4 * g : P, a:b],
+                    start=(i == 0),
+                    stop=(i == len(runs) - 1),
+                )
+            nc.scalar.activation(h[t][:, c0:c1], acc[:], SILU)
 
         rounded_tile("w1_00", [(0, 0)])
         rounded_tile("w1_01", [(0, 1)])
@@ -196,13 +197,18 @@ def tile_picked_lapl_silu_p_kernel(
         round_w1("w1_01", 0, 1, 1, nc.scalar.copy)
         round_w1("w1_1", 1, 2, 0, nc.scalar.copy)
         round_w1("w1_1", 1, 2, 1, nc.scalar.copy)
-        pick(0, 0, S, 1, "picked0")
+        pick(0, 0, S, "picked0")
         quantize_w1("w1_00")
-        pick(1, 0, BANK, 1, "picked1_0")
+        pick(1, 0, 512, "picked1_0")
         quantize_w1("w1_01")
-        pick(1, BANK, S, 2, "w1_01")
-        first_layer(0, ((0, 512, 0), (512, 768, 1), (768, 1024, 7)))
+        pick(1, 512, 768, "w1_01")
         quantize_w1("w1_1")
+        pick(1, 768, 1024, "w1_1")
+        first_layer(0, 0, 512, 0)
+        first_layer(0, 512, 768, 1)
+        first_layer(1, 0, 512, 2)
+        first_layer(0, 768, 1024, 7)
+        first_layer(1, 512, 1024, 3)
         round_w1("w1_23", 2, 4, 0, nc.vector.tensor_copy)
         round_w1("w1_23", 2, 4, 1, nc.vector.tensor_copy)
         quantize_w1("w1_23")
@@ -234,15 +240,15 @@ def tile_picked_lapl_silu_p_kernel(
 
         def add_terms(t, b0, b1, number):
             acc = bank(number, [P, b1 - b0, P], "z_acc")
-            for b in range(b0, b1):
-                for i, name in enumerate(("own", 0, 1)):
+            for i, name in enumerate(("own", 0, 1)):
+                for b in range(b0, b1):
                     nc.tensor.matmul(
                         acc[:, b - b0, :],
                         lhsT=terms[name, t, b],
                         rhs=identity[:],
                         is_transpose=True,
-                        start=(i == 0),
-                        stop=(i == 2),
+                        start=(i == 0 and b == b0),
+                        stop=(i == 2 and b == b1 - 1),
                     )
             sums[t, b0] = acc
 
@@ -276,7 +282,7 @@ def tile_picked_lapl_silu_p_kernel(
             nc.vector.quantize_mx(out=codes[:].bitcast(FP8X4), scales=plane[:], in_=z_grouped[b0][:])
             z_mx[b0] = (codes, plane)
 
-        def second_layer(b0, b1, number, copy):
+        def second_layer(b0, b1, number, copy, queue):
             width = (b1 - b0) * P
             codes, plane = z_mx[b0]
             acc = bank(number, [P, width], "out_acc")
@@ -291,13 +297,14 @@ def tile_picked_lapl_silu_p_kernel(
             )
             result = keep.tile([P, width], F32, name=f"result{b0}")
             copy(result[:], acc[:])
-            nc.sync.dma_start(out[:, b0 * P : b1 * P], result[:])
+            queue.dma_start(out[:, b0 * P : b1 * P], result[:])
 
         on_scalar, on_vector = nc.scalar.copy, nc.vector.tensor_copy
-        first_layer(1, ((0, 512, 2), (512, 1024, 3)))
         centres(0, 0, 4)
-        first_layer(2, ((0, 512, 4), (512, 1024, 5)))
-        first_layer(3, ((0, 512, 0), (512, 1024, 1)))
+        first_layer(2, 0, 512, 4)
+        first_layer(2, 512, 1024, 5)
+        first_layer(3, 0, 512, 0)
+        first_layer(3, 512, 1024, 1)
         both0 = placed.tile([P, 2 * V], F32, name="both0", offset=0)
         both1 = placed.tile([P, 2 * V], F32, name="both1", offset=4096)
         neighbours(0, 0, 0, 4, both0[:, 0:V])
@@ -333,12 +340,12 @@ def tile_picked_lapl_silu_p_kernel(
         neighbours(1, 3, 3, 4)
         add_terms(3, 3, 4, 4)
         round_z(3, 2, 2, 3, on_scalar)
-        round_z(3, 3, 3, 4, on_vector)
+        round_z(3, 3, 3, 4, on_scalar)
         quantize_z(0, 2)
         turn_back(2, 3, (5,), on_scalar)
-        turn_back(3, 4, (6,), on_vector)
-        second_layer(0, 2, 7, on_scalar)
+        turn_back(3, 4, (6,), on_scalar)
+        second_layer(0, 2, 4, on_vector, nc.sync)
         quantize_z(2, 3)
         quantize_z(3, 4)
-        second_layer(2, 3, 0, on_scalar)
-        second_layer(3, 4, 2, on_vector)
+        second_layer(2, 3, 0, on_vector, nc.sync)
+        second_layer(3, 4, 2, on_scalar, nc.scalar)

@@ -37,7 +37,6 @@ def tile_picked_lapl_silu_p_kernel(
     with ExitStack() as ctx:
         lists = ctx.enter_context(tc.tile_pool(name="lists", bufs=1))
         keep = ctx.enter_context(tc.tile_pool(name="keep", bufs=1))
-        placed = ctx.enter_context(tc.tile_pool(name="placed", bufs=1))
         psum = ctx.enter_context(tc.psum_pool(name="psum", bufs=1))
 
         def bank(number, shape, name):
@@ -63,7 +62,7 @@ def tile_picked_lapl_silu_p_kernel(
 
         def load_w1(tiles, g):
             t0, t1 = tiles
-            raw = keep.tile([P, PACK, (t1 - t0) * P], F32, name=f"w1_raw{t0}_{g}")
+            raw = keep.tile([P, PACK, (t1 - t0) * P], F32, name=f"w1_raw{t0}_{g}", tag=f"w1_raw{t0}_{g}", align_bytes=64)
             rows = w1[g * P * PACK : (g + 1) * P * PACK, t0 * P : t1 * P]
             nc.sync.dma_start(raw[:], rows.rearrange("(p j) c -> p j c", j=PACK))
             for t in range(t0, t1):
@@ -138,12 +137,8 @@ def tile_picked_lapl_silu_p_kernel(
         w1_grouped = {}
         w1_mx = {}
 
-        def rounded_tile(name, parts, offset=None):
-            shape = [P, len(parts) * P * PACK]
-            if offset is None:
-                tile = keep.tile(shape, BF16, name=name, tag=name, align_bytes=64)
-            else:
-                tile = placed.tile(shape, BF16, name=name, offset=offset, align_bytes=64)
+        def rounded_tile(name, parts):
+            tile = keep.tile([P, len(parts) * P * PACK], BF16, name=name, tag=name, align_bytes=64)
             w1_grouped[name] = (tile, parts)
 
         def round_w1(name, t0, t1, g, copy):
@@ -192,7 +187,9 @@ def tile_picked_lapl_silu_p_kernel(
         rounded_tile("w1_00", [(0, 0)])
         rounded_tile("w1_01", [(0, 1)])
         rounded_tile("w1_1", [(1, 0), (1, 1)])
-        rounded_tile("w1_23", [(2, 0), (3, 0), (2, 1), (3, 1)], 2048)
+        rounded_tile("w1_a", [(2, 0), (3, 0)])
+        rounded_tile("w1_21", [(2, 1)])
+        rounded_tile("w1_31", [(3, 1)])
         round_w1("w1_00", 0, 1, 0, nc.scalar.copy)
         round_w1("w1_01", 0, 1, 1, nc.scalar.copy)
         round_w1("w1_1", 1, 2, 0, nc.scalar.copy)
@@ -201,17 +198,16 @@ def tile_picked_lapl_silu_p_kernel(
         quantize_w1("w1_00")
         pick(1, 0, 512, "picked1_0")
         quantize_w1("w1_01")
-        pick(1, 512, 768, "w1_01")
-        quantize_w1("w1_1")
-        pick(1, 768, 1024, "w1_1")
+        pick(1, 512, 768, "w1_raw0_1")
+        pick(1, 768, 1024, "picked1_768")
         first_layer(0, 0, 512, 0)
-        first_layer(0, 512, 768, 1)
-        first_layer(1, 0, 512, 2)
         first_layer(0, 768, 1024, 7)
+        first_layer(0, 512, 768, 1)
+        quantize_w1("w1_1")
+        first_layer(1, 0, 512, 2)
         first_layer(1, 512, 1024, 3)
-        round_w1("w1_23", 2, 4, 0, nc.vector.tensor_copy)
-        round_w1("w1_23", 2, 4, 1, nc.vector.tensor_copy)
-        quantize_w1("w1_23")
+        round_w1("w1_a", 2, 4, 0, nc.vector.tensor_copy)
+        quantize_w1("w1_a")
 
         z_rows = keep.tile([P, BLOCKS * H], BF16, name="z_rows", align_bytes=64)
         z_view = z_rows[:].rearrange("v (b u p e) -> v b u p e", b=BLOCKS, u=2, e=2)
@@ -301,16 +297,20 @@ def tile_picked_lapl_silu_p_kernel(
 
         on_scalar, on_vector = nc.scalar.copy, nc.vector.tensor_copy
         centres(0, 0, 4)
+        first0 = keep.tile([P, V], F32, name="first0", tag="w1_raw2_0", align_bytes=64)
+        neighbours(0, 0, 0, 4, first0)
+        round_w1("w1_21", 2, 3, 1, nc.vector.tensor_copy)
+        round_w1("w1_31", 3, 4, 1, nc.vector.tensor_copy)
+        quantize_w1("w1_21")
+        quantize_w1("w1_31")
         first_layer(2, 0, 512, 4)
         first_layer(2, 512, 1024, 5)
         first_layer(3, 0, 512, 0)
         first_layer(3, 512, 1024, 1)
-        both0 = placed.tile([P, 2 * V], F32, name="both0", offset=0)
-        both1 = placed.tile([P, 2 * V], F32, name="both1", offset=4096)
-        neighbours(0, 0, 0, 4, both0[:, 0:V])
-        neighbours(1, 0, 0, 4, both0[:, V : 2 * V])
-        neighbours(0, 1, 0, 4, both1[:, 0:V])
-        neighbours(1, 1, 0, 4, both1[:, V : 2 * V])
+        later = keep.tile([P, 3 * V], F32, name="later", tag="w1_21", align_bytes=64)
+        neighbours(1, 0, 0, 4, later[:, 0:V])
+        neighbours(0, 1, 0, 4, later[:, V : 2 * V])
+        neighbours(1, 1, 0, 4, later[:, 2 * V : 3 * V])
         add_terms(0, 0, 4, 4)
         centres(1, 0, 4)
         centres(2, 0, 4)

@@ -234,9 +234,9 @@ def tile_picked_lapl_silu_p_kernel(
             nc.vector.tensor_tensor(term[:], h[t][:].indirect(offsets), edge_weights[d, weights][:, b0 * P : b1 * P], MULT)
             keep_terms(d, t, b0, b1, term)
 
-        def add_terms(t, b0, b1, number):
+        def add_terms(t, b0, b1, number, names=("own", 0, 1)):
             acc = bank(number, [P, b1 - b0, P], "z_acc")
-            for i, name in enumerate(("own", 0, 1)):
+            for i, name in enumerate(names):
                 for b in range(b0, b1):
                     nc.tensor.matmul(
                         acc[:, b - b0, :],
@@ -311,41 +311,41 @@ def tile_picked_lapl_silu_p_kernel(
         neighbours(1, 0, 0, 4, later[:, 0:V])
         neighbours(0, 1, 0, 4, later[:, V : 2 * V])
         neighbours(1, 1, 0, 4, later[:, 2 * V : 3 * V])
-        add_terms(0, 0, 4, 4)
+        add_terms(0, 0, 4, 6, (0, "own", 1))
         centres(1, 0, 4)
         centres(2, 0, 4)
-        add_terms(1, 0, 4, 5)
+        add_terms(1, 0, 4, 7)
         centres(3, 0, 2)
         round_z(0, 0, 0, 4, on_scalar)
         round_z(1, 0, 0, 4, on_scalar)
         neighbours(0, 2, 0, 2)
         neighbours(1, 2, 0, 2)
-        add_terms(2, 0, 2, 6)
+        add_terms(2, 0, 2, 2, (0, "own", 1))
         neighbours(0, 3, 0, 2, None, "early")
         neighbours(1, 3, 0, 2, None, "early")
-        add_terms(3, 0, 2, 7)
+        add_terms(3, 0, 2, 3)
         round_z(2, 0, 0, 2, on_scalar)
         round_z(3, 0, 0, 2, on_scalar)
         centres(3, 2, 4)
         for d in range(NEIGHBOURS):
             late = keep.tile([P, V // 2], F32, name=f"late{d}", tag=f"early_weights{d}")
             neighbours(d, 2, 2, 4, late)
-        add_terms(2, 2, 4, 0)
+        add_terms(2, 2, 4, 4)
         round_z(2, 2, 2, 4, on_scalar)
-        turn_back(0, 2, (2, 3), on_scalar)
+        turn_back(0, 2, (5, 0), on_scalar)
         neighbours(0, 3, 2, 3)
         neighbours(1, 3, 2, 3)
         add_terms(3, 2, 3, 1)
         neighbours(0, 3, 3, 4)
         neighbours(1, 3, 3, 4)
-        add_terms(3, 3, 4, 4)
+        add_terms(3, 3, 4, 6)
         round_z(3, 2, 2, 3, on_scalar)
         round_z(3, 3, 3, 4, on_scalar)
         quantize_z(0, 2)
-        turn_back(2, 3, (5,), on_scalar)
-        turn_back(3, 4, (6,), on_scalar)
-        second_layer(0, 2, 4, on_vector, nc.sync)
+        turn_back(2, 3, (7,), on_scalar)
+        turn_back(3, 4, (2,), on_scalar)
+        second_layer(0, 2, 6, on_vector, nc.sync)
         quantize_z(2, 3)
         quantize_z(3, 4)
-        second_layer(2, 3, 0, on_vector, nc.sync)
-        second_layer(3, 4, 2, on_scalar, nc.scalar)
+        second_layer(2, 3, 3, on_vector, nc.sync)
+        second_layer(3, 4, 4, on_scalar, nc.scalar)

@@ -42,16 +42,41 @@ def tile_picked_lapl_silu_p_kernel(
         def bank(number, shape, name):
             return psum.tile(shape, F32, name=name, tag=f"bank{number}")
 
-        x_plane = keep.tile([P, T], U8, name="x_plane", align_bytes=64)
-        nc.gpsimd.memset(x_plane[:].bitcast(I32), 0)
+        placed = ctx.enter_context(tc.tile_pool(name="placed", bufs=1))
+        offsets_of = {
+            "w1_raw0_1": 0,
+            "picked1_768": 0,
+            "x_rows": 1984,
+            "w1_raw1_0": 3968,
+            "later": 1024,
+            "w1_raw2_1": 6016,
+            "x_table0": 10048,
+            "w2_codes": 10112,
+            "w2_plane": 10368,
+            "h0": 16128,
+            "w1_raw1_1": 18240,
+            "gate_cols": 20224,
+            "w1_00": 20288,
+            "w1_raw2_0": 21312,
+            "first0": 21312,
+            "w1_raw0_0": 25408,
+            "picked1_0": 25408,
+        }
+
+        def tile_for(shape, dtype, name):
+            if name in offsets_of:
+                return placed.tile(shape, dtype, name=name, offset=offsets_of[name], align_bytes=64)
+            return keep.tile(shape, dtype, name=name, tag=name, align_bytes=64)
+
         gate_rows = keep.tile([P, P], F32, name="gate_rows")
         nc.gpsimd.memset(gate_rows[:], 0.0)
         warm_in = keep.tile([P, 1], F32, name="warm_in")
         warm_out = keep.tile([P, 1], F32, name="warm_out")
         nc.gpsimd.memset(warm_in[:], 0.0)
         nc.scalar.activation(warm_out[:], warm_in[:], SILU)
-        w2_plane = keep.tile([P, N], U8, name="w2_plane", align_bytes=64)
-        nc.gpsimd.memset(w2_plane[:].bitcast(I32), 0)
+        x_rows = tile_for([P, T], U8, "x_rows")
+        nc.gpsimd.memset(x_rows[32:64, :].bitcast(I32), 0)
+        nc.gpsimd.memset(x_rows[64:P, :].bitcast(I32), 0)
 
         def load_list(name, source, entries):
             tile = lists.tile([P, entries // PER_COLUMN], U16, name=name)
@@ -62,7 +87,7 @@ def tile_picked_lapl_silu_p_kernel(
 
         def load_w1(tiles, g):
             t0, t1 = tiles
-            raw = keep.tile([P, PACK, (t1 - t0) * P], F32, name=f"w1_raw{t0}_{g}", tag=f"w1_raw{t0}_{g}", align_bytes=64)
+            raw = tile_for([P, PACK, (t1 - t0) * P], F32, f"w1_raw{t0}_{g}")
             rows = w1[g * P * PACK : (g + 1) * P * PACK, t0 * P : t1 * P]
             nc.sync.dma_start(raw[:], rows.rearrange("(p j) c -> p j c", j=PACK))
             for t in range(t0, t1):
@@ -71,48 +96,42 @@ def tile_picked_lapl_silu_p_kernel(
         x_table = []
 
         def load_x(g):
-            table = keep.tile([P, T], I32, name=f"x_table{g}", align_bytes=64)
+            table = tile_for([P, T], I32, f"x_table{g}")
             nc.sync.dma_start(table[:], x_words[g].rearrange("p n t -> p (n t)").bitcast(I32))
             x_table.append(table)
 
         offs_sb = load_list("offs_sb", offs, S)
-        for q in range(QUADRANTS):
-            nc.sync.dma_start(
-                x_plane[32 * q : 32 * q + 4 * PASSES, :].bitcast(I32),
-                x_scales[:, 4 * q : 4 * q + 4, :].bitcast(I32),
-            )
-        cen_sb = load_list("cen_sb", cen, V)
+        rows_by_r = x_scales.bitcast(I32).rearrange("g (q r) n -> r q g n", r=4)
+        for r in range(4):
+            nc.sync.dma_start(x_rows[r:32:4, :].bitcast(I32), rows_by_r[r])
         nc.sync.dma_start(
             gate_rows[0 : NEIGHBOURS * BLOCKS, :], gate[:, 0, :].rearrange("d (b k) -> d b k", k=P)
         )
         load_x(0)
         pos1_sb = load_list("pos1_sb", pos1, V)
         load_w1(W1_LOADS[0], 0)
-        load_x(1)
-        load_w1(W1_LOADS[0], 1)
-        for g in range(PASSES):
-            load_w1(W1_LOADS[1], g)
+        cen_sb = load_list("cen_sb", cen, V)
         pos2_sb = load_list("pos2_sb", pos2, V)
-        for g in range(PASSES):
-            load_w1(W1_LOADS[2], g)
-        w2_codes = keep.tile([P, 2 * N], U8, name="w2_codes", align_bytes=64)
-        nc.sync.dma_start(w2_codes[:].bitcast(I32), w2_words[0].bitcast(I32))
-        for q in range(QUADRANTS):
-            nc.sync.dma_start(
-                w2_plane[32 * q : 32 * q + 4, :].bitcast(I32),
-                w2_scales[0, 4 * q : 4 * q + 4, :].bitcast(I32),
-            )
+        load_x(1)
 
         identity = keep.tile([P, P], F32, name="identity")
         make_identity(nc, identity[:])
-
         picked_plane = keep.tile([P, S], U8, name="picked_plane", align_bytes=64)
-        nc.vector.tensor_copy(picked_plane[:], x_plane[:].indirect(offs_sb[:]))
+        nc.gpsimd.memset(picked_plane[:].bitcast(I32), 0)
+
+        picked_rows = keep.tile([P, S], U8, name="picked_rows", align_bytes=64)
+        nc.vector.tensor_copy(picked_rows[:], x_rows[:].indirect(offs_sb[:]))
+        for q in range(QUADRANTS):
+            nc.sync.dma_start(
+                picked_plane[32 * q : 32 * q + 8, :].bitcast(I32), picked_rows[8 * q : 8 * q + 8, :].bitcast(I32)
+            )
+        load_w1(W1_LOADS[0], 1)
+        load_w1(W1_LOADS[1], 0)
 
         gate_turned = bank(2, [P, P], "gate_turned")
         nc.tensor.transpose(gate_turned[:], gate_rows[:], identity[:])
-        gate_cols = keep.tile([P, NEIGHBOURS * BLOCKS], F32, name="gate_cols")
-        nc.scalar.copy(gate_cols[:], gate_turned[:, 0 : NEIGHBOURS * BLOCKS])
+        gate_cols = tile_for([P, 288], F32, "gate_cols")
+        nc.scalar.copy(gate_cols[:, 0 : NEIGHBOURS * BLOCKS], gate_turned[:, 0 : NEIGHBOURS * BLOCKS])
         edge_weights = {}
         for d in range(NEIGHBOURS):
             spread = bank(3 + d, [P, BLOCKS, P], "spread")
@@ -125,20 +144,25 @@ def tile_picked_lapl_silu_p_kernel(
             early = keep.tile([P, V // 2], F32, name=f"early_weights{d}", tag=f"early_weights{d}")
             nc.scalar.activation(early[:], spread[:, 0:2, :].rearrange("p b k -> p (b k)"), COPY, scale=-1.0)
             edge_weights[d, "early"] = early
+            if d == 0:
+                first = keep.tile([P, V // 2], F32, name="first_weights", tag="w1_b", align_bytes=64)
+                nc.scalar.activation(first[:], spread[:, 0:2, :].rearrange("p b k -> p (b k)"), COPY, scale=-1.0)
+                edge_weights[d, "first"] = first
 
         picked = {0: [], 1: []}
 
-        def pick(g, e0, e1, tag):
-            words = keep.tile([P, e1 - e0], U32, name=f"picked{g}_{e0}", tag=tag, align_bytes=64)
-            offsets = offs_sb[:, e0 // PER_COLUMN : e1 // PER_COLUMN]
-            nc.vector.tensor_copy(words[:], x_table[g][:].bitcast(U32).indirect(offsets))
+        def pick(g, e0, e1, borders):
+            words = tile_for([P, e1 - e0], U32, f"picked{g}_{e0}")
+            for a, b in zip(borders, borders[1:]):
+                offsets = offs_sb[:, a // PER_COLUMN : b // PER_COLUMN]
+                nc.vector.tensor_copy(words[:, a - e0 : b - e0], x_table[g][:].bitcast(U32).indirect(offsets))
             picked[g].append((e0, e1, words))
 
         w1_grouped = {}
         w1_mx = {}
 
         def rounded_tile(name, parts):
-            tile = keep.tile([P, len(parts) * P * PACK], BF16, name=name, tag=name, align_bytes=64)
+            tile = tile_for([P, len(parts) * P * PACK], BF16, name)
             w1_grouped[name] = (tile, parts)
 
         def round_w1(name, t0, t1, g, copy):
@@ -150,12 +174,14 @@ def tile_picked_lapl_silu_p_kernel(
                 raw[:, :, (t0 - base) * P : (t1 - base) * P].rearrange("p j (c i) -> p c j i", i=PACK),
             )
 
-        def quantize_w1(name, tag=None):
+        def quantize_w1(name, first=0, end=None):
             tile, parts = w1_grouped[name]
+            parts = parts[first:end]
             width = len(parts) * P
-            codes = keep.tile([P, width], U32, name=f"{name}_codes", tag=tag or f"{name}_codes", align_bytes=64)
-            plane = keep.tile([P, width], U8, name=f"{name}_plane", align_bytes=64)
-            nc.vector.quantize_mx(out=codes[:].bitcast(FP8X4), scales=plane[:], in_=tile[:])
+            codes = keep.tile([P, width], U32, name=f"{name}_codes{first}", align_bytes=64)
+            plane = keep.tile([P, width], U8, name=f"{name}_plane{first}", align_bytes=64)
+            source = tile[:, first * P * PACK : first * P * PACK + width * PACK]
+            nc.vector.quantize_mx(out=codes[:].bitcast(FP8X4), scales=plane[:], in_=source)
             for i, part in enumerate(parts):
                 w1_mx[part] = (codes[:, i * P : (i + 1) * P], plane[:, i * P : (i + 1) * P])
 
@@ -163,7 +189,7 @@ def tile_picked_lapl_silu_p_kernel(
 
         def first_layer(t, c0, c1, number):
             if t not in h:
-                h[t] = keep.tile([P, S], F32, name=f"h{t}")
+                h[t] = tile_for([P, S], F32, f"h{t}")
             acc = bank(number, [P, c1 - c0], "h_acc")
             runs = [
                 (g, max(c0, e0), min(c1, e1), e0, words)
@@ -188,21 +214,30 @@ def tile_picked_lapl_silu_p_kernel(
         rounded_tile("w1_01", [(0, 1)])
         rounded_tile("w1_1", [(1, 0), (1, 1)])
         rounded_tile("w1_a", [(2, 0), (3, 0)])
-        rounded_tile("w1_21", [(2, 1)])
-        rounded_tile("w1_31", [(3, 1)])
         round_w1("w1_00", 0, 1, 0, nc.scalar.copy)
+        load_w1(W1_LOADS[1], 1)
+        load_w1(W1_LOADS[2], 0)
         round_w1("w1_01", 0, 1, 1, nc.scalar.copy)
         round_w1("w1_1", 1, 2, 0, nc.scalar.copy)
+        pick(0, 0, S, (0, S))
         round_w1("w1_1", 1, 2, 1, nc.scalar.copy)
-        pick(0, 0, S, "picked0")
         quantize_w1("w1_00")
-        pick(1, 0, 512, "picked1_0")
+        load_w1(W1_LOADS[2], 1)
+        w2_codes = tile_for([P, 2 * N], U8, "w2_codes")
+        nc.sync.dma_start(w2_codes[:].bitcast(I32), w2_words[0].bitcast(I32))
+        w2_plane = tile_for([P, N], U8, "w2_plane")
+        nc.vector.memset(w2_plane[:].bitcast(I32), 0)
+        for q in range(QUADRANTS):
+            nc.sync.dma_start(
+                w2_plane[32 * q : 32 * q + 4, :].bitcast(I32),
+                w2_scales[0, 4 * q : 4 * q + 4, :].bitcast(I32),
+            )
+        pick(1, 0, 768, (0, 512, 768))
         quantize_w1("w1_01")
-        pick(1, 512, 768, "w1_raw0_1")
-        pick(1, 768, 1024, "picked1_768")
+        pick(1, 768, 1024, (768, 1024))
         first_layer(0, 0, 512, 0)
-        first_layer(0, 768, 1024, 7)
         first_layer(0, 512, 768, 1)
+        first_layer(0, 768, 1024, 7)
         quantize_w1("w1_1")
         first_layer(1, 0, 512, 2)
         first_layer(1, 512, 1024, 3)
@@ -297,17 +332,19 @@ def tile_picked_lapl_silu_p_kernel(
 
         on_scalar, on_vector = nc.scalar.copy, nc.vector.tensor_copy
         centres(0, 0, 4)
-        first0 = keep.tile([P, V], F32, name="first0", tag="w1_raw2_0", align_bytes=64)
-        neighbours(0, 0, 0, 4, first0)
-        round_w1("w1_21", 2, 3, 1, nc.vector.tensor_copy)
-        round_w1("w1_31", 3, 4, 1, nc.vector.tensor_copy)
-        quantize_w1("w1_21")
-        quantize_w1("w1_31")
+        first0 = tile_for([P, V], F32, "first0")
+        neighbours(0, 0, 0, 2, first0[:, 0 : V // 2], "first")
+        neighbours(0, 0, 2, 4, first0[:, V // 2 : V])
+        rounded_tile("w1_b", [(2, 1), (3, 1)])
+        round_w1("w1_b", 2, 3, 1, nc.vector.tensor_copy)
+        round_w1("w1_b", 3, 4, 1, nc.vector.tensor_copy)
+        quantize_w1("w1_b", 0, 1)
+        quantize_w1("w1_b", 1, 2)
         first_layer(2, 0, 512, 4)
         first_layer(2, 512, 1024, 5)
         first_layer(3, 0, 512, 0)
         first_layer(3, 512, 1024, 1)
-        later = keep.tile([P, 3 * V], F32, name="later", tag="w1_21", align_bytes=64)
+        later = tile_for([P, 3 * V], F32, "later")
         neighbours(1, 0, 0, 4, later[:, 0:V])
         neighbours(0, 1, 0, 4, later[:, V : 2 * V])
         neighbours(1, 1, 0, 4, later[:, 2 * V : 3 * V])

@@ -44,23 +44,23 @@ def tile_picked_lapl_silu_p_kernel(
 
         placed = ctx.enter_context(tc.tile_pool(name="placed", bufs=1))
         offsets_of = {
-            "w1_raw0_1": 0,
-            "picked1_768": 0,
             "x_rows": 1984,
             "w1_raw1_0": 3968,
-            "later": 1024,
+            "h0": 1920,
             "w1_raw2_1": 6016,
+            "later": 6016,
             "x_table0": 10048,
-            "w2_codes": 10112,
-            "w2_plane": 10368,
-            "h0": 16128,
+            "w2_codes": 12160,
+            "w2_plane": 12416,
             "w1_raw1_1": 18240,
             "gate_cols": 20224,
             "w1_00": 20288,
             "w1_raw2_0": 21312,
             "first0": 21312,
             "w1_raw0_0": 25408,
-            "picked1_0": 25408,
+            "picked1_512": 25408,
+            "w1_raw0_1": 27456,
+            "picked1_768": 27456,
         }
 
         def tile_for(shape, dtype, name):
@@ -101,18 +101,19 @@ def tile_picked_lapl_silu_p_kernel(
             x_table.append(table)
 
         offs_sb = load_list("offs_sb", offs, S)
-        rows_by_r = x_scales.bitcast(I32).rearrange("g (q r) n -> r q g n", r=4)
-        for r in range(4):
-            nc.sync.dma_start(x_rows[r:32:4, :].bitcast(I32), rows_by_r[r])
+        for g in range(PASSES):
+            rows = x_scales[g].bitcast(I32).rearrange("(q r) n -> r q n", r=4)
+            nc.sync.dma_start(x_rows[16 * g : 16 * (g + 1), :].bitcast(I32), rows)
         nc.sync.dma_start(
             gate_rows[0 : NEIGHBOURS * BLOCKS, :], gate[:, 0, :].rearrange("d (b k) -> d b k", k=P)
         )
         load_x(0)
         pos1_sb = load_list("pos1_sb", pos1, V)
-        load_w1(W1_LOADS[0], 0)
         cen_sb = load_list("cen_sb", cen, V)
         pos2_sb = load_list("pos2_sb", pos2, V)
         load_x(1)
+        for g in range(PASSES):
+            load_w1(W1_LOADS[0], g)
 
         identity = keep.tile([P, P], F32, name="identity")
         make_identity(nc, identity[:])
@@ -123,9 +124,8 @@ def tile_picked_lapl_silu_p_kernel(
         nc.vector.tensor_copy(picked_rows[:], x_rows[:].indirect(offs_sb[:]))
         for q in range(QUADRANTS):
             nc.sync.dma_start(
-                picked_plane[32 * q : 32 * q + 8, :].bitcast(I32), picked_rows[8 * q : 8 * q + 8, :].bitcast(I32)
+                picked_plane[32 * q : 32 * q + 8, :].bitcast(I32), picked_rows[q:32:4, :].bitcast(I32)
             )
-        load_w1(W1_LOADS[0], 1)
         load_w1(W1_LOADS[1], 0)
 
         gate_turned = bank(2, [P, P], "gate_turned")
@@ -220,7 +220,7 @@ def tile_picked_lapl_silu_p_kernel(
         round_w1("w1_01", 0, 1, 1, nc.scalar.copy)
         round_w1("w1_1", 1, 2, 0, nc.scalar.copy)
         pick(0, 0, S, (0, S))
-        round_w1("w1_1", 1, 2, 1, nc.scalar.copy)
+        pick(1, 0, 512, (0, 512))
         quantize_w1("w1_00")
         load_w1(W1_LOADS[2], 1)
         w2_codes = tile_for([P, 2 * N], U8, "w2_codes")
@@ -232,17 +232,17 @@ def tile_picked_lapl_silu_p_kernel(
                 w2_plane[32 * q : 32 * q + 4, :].bitcast(I32),
                 w2_scales[0, 4 * q : 4 * q + 4, :].bitcast(I32),
             )
-        pick(1, 0, 768, (0, 512, 768))
+        pick(1, 512, 768, (512, 768))
         quantize_w1("w1_01")
         pick(1, 768, 1024, (768, 1024))
         first_layer(0, 0, 512, 0)
         first_layer(0, 512, 768, 1)
         first_layer(0, 768, 1024, 7)
+        round_w1("w1_1", 1, 2, 1, nc.vector.tensor_copy)
         quantize_w1("w1_1")
         first_layer(1, 0, 512, 2)
         first_layer(1, 512, 1024, 3)
         round_w1("w1_a", 2, 4, 0, nc.vector.tensor_copy)
-        quantize_w1("w1_a")
 
         z_rows = keep.tile([P, BLOCKS * H], BF16, name="z_rows", align_bytes=64)
         z_view = z_rows[:].rearrange("v (b u p e) -> v b u p e", b=BLOCKS, u=2, e=2)
@@ -336,10 +336,9 @@ def tile_picked_lapl_silu_p_kernel(
         neighbours(0, 0, 0, 2, first0[:, 0 : V // 2], "first")
         neighbours(0, 0, 2, 4, first0[:, V // 2 : V])
         rounded_tile("w1_b", [(2, 1), (3, 1)])
-        round_w1("w1_b", 2, 3, 1, nc.vector.tensor_copy)
-        round_w1("w1_b", 3, 4, 1, nc.vector.tensor_copy)
-        quantize_w1("w1_b", 0, 1)
-        quantize_w1("w1_b", 1, 2)
+        round_w1("w1_b", 2, 4, 1, nc.vector.tensor_copy)
+        quantize_w1("w1_a")
+        quantize_w1("w1_b")
         first_layer(2, 0, 512, 4)
         first_layer(2, 512, 1024, 5)
         first_layer(3, 0, 512, 0)

@@ -44,19 +44,17 @@ def tile_picked_lapl_silu_p_kernel(
 
         placed = ctx.enter_context(tc.tile_pool(name="placed", bufs=1))
         offsets_of = {
+            "w1_raw1_1": 0,
             "x_rows": 1984,
             "w1_raw1_0": 3968,
-            "h0": 1920,
-            "w1_raw2_1": 6016,
-            "later": 6016,
-            "x_table0": 10048,
-            "w2_codes": 12160,
-            "w2_plane": 12416,
-            "w1_raw1_1": 18240,
-            "gate_cols": 20224,
-            "w1_00": 20288,
-            "w1_raw2_0": 21312,
-            "first0": 21312,
+            "h0": 3968,
+            "w1_raw2_1": 8064,
+            "later": 8064,
+            "x_table0": 12096,
+            "w2_codes": 14208,
+            "w2_plane": 14464,
+            "w1_raw2_0": 14592,
+            "first0": 14592,
             "w1_raw0_0": 25408,
             "picked1_512": 25408,
             "w1_raw0_1": 27456,
@@ -126,12 +124,13 @@ def tile_picked_lapl_silu_p_kernel(
             nc.sync.dma_start(
                 picked_plane[32 * q : 32 * q + 8, :].bitcast(I32), picked_rows[q:32:4, :].bitcast(I32)
             )
-        load_w1(W1_LOADS[1], 0)
+        for g in range(PASSES):
+            load_w1(W1_LOADS[1], g)
 
         gate_turned = bank(2, [P, P], "gate_turned")
         nc.tensor.transpose(gate_turned[:], gate_rows[:], identity[:])
-        gate_cols = tile_for([P, 288], F32, "gate_cols")
-        nc.scalar.copy(gate_cols[:, 0 : NEIGHBOURS * BLOCKS], gate_turned[:, 0 : NEIGHBOURS * BLOCKS])
+        gate_cols = keep.tile([P, NEIGHBOURS * BLOCKS], F32, name="gate_cols", tag="w1_00", align_bytes=64)
+        nc.scalar.copy(gate_cols[:], gate_turned[:, 0 : NEIGHBOURS * BLOCKS])
         edge_weights = {}
         for d in range(NEIGHBOURS):
             spread = bank(3 + d, [P, BLOCKS, P], "spread")
@@ -144,10 +143,6 @@ def tile_picked_lapl_silu_p_kernel(
             early = keep.tile([P, V // 2], F32, name=f"early_weights{d}", tag=f"early_weights{d}")
             nc.scalar.activation(early[:], spread[:, 0:2, :].rearrange("p b k -> p (b k)"), COPY, scale=-1.0)
             edge_weights[d, "early"] = early
-            if d == 0:
-                first = keep.tile([P, V // 2], F32, name="first_weights", tag="w1_b", align_bytes=64)
-                nc.scalar.activation(first[:], spread[:, 0:2, :].rearrange("p b k -> p (b k)"), COPY, scale=-1.0)
-                edge_weights[d, "first"] = first
 
         picked = {0: [], 1: []}
 
@@ -178,7 +173,7 @@ def tile_picked_lapl_silu_p_kernel(
             tile, parts = w1_grouped[name]
             parts = parts[first:end]
             width = len(parts) * P
-            codes = keep.tile([P, width], U32, name=f"{name}_codes{first}", align_bytes=64)
+            codes = tile_for([P, width], U32, f"{name}_codes{first}")
             plane = keep.tile([P, width], U8, name=f"{name}_plane{first}", align_bytes=64)
             source = tile[:, first * P * PACK : first * P * PACK + width * PACK]
             nc.vector.quantize_mx(out=codes[:].bitcast(FP8X4), scales=plane[:], in_=source)
@@ -213,16 +208,15 @@ def tile_picked_lapl_silu_p_kernel(
         rounded_tile("w1_00", [(0, 0)])
         rounded_tile("w1_01", [(0, 1)])
         rounded_tile("w1_1", [(1, 0), (1, 1)])
-        rounded_tile("w1_a", [(2, 0), (3, 0)])
+        rounded_tile("w1_23", [(2, 0), (2, 1), (3, 0), (3, 1)])
         round_w1("w1_00", 0, 1, 0, nc.scalar.copy)
-        load_w1(W1_LOADS[1], 1)
-        load_w1(W1_LOADS[2], 0)
         round_w1("w1_01", 0, 1, 1, nc.scalar.copy)
         round_w1("w1_1", 1, 2, 0, nc.scalar.copy)
         pick(0, 0, S, (0, S))
         pick(1, 0, 512, (0, 512))
         quantize_w1("w1_00")
-        load_w1(W1_LOADS[2], 1)
+        for g in range(PASSES):
+            load_w1(W1_LOADS[2], g)
         w2_codes = tile_for([P, 2 * N], U8, "w2_codes")
         nc.sync.dma_start(w2_codes[:].bitcast(I32), w2_words[0].bitcast(I32))
         w2_plane = tile_for([P, N], U8, "w2_plane")
@@ -242,7 +236,10 @@ def tile_picked_lapl_silu_p_kernel(
         quantize_w1("w1_1")
         first_layer(1, 0, 512, 2)
         first_layer(1, 512, 1024, 3)
-        round_w1("w1_a", 2, 4, 0, nc.vector.tensor_copy)
+        nc.vector.tensor_copy(
+            w1_grouped["w1_23"][0][:].rearrange("p (t g c i j) -> p g t c j i", t=2, g=PASSES, i=PACK, j=PACK)[:, 0],
+            w1_raw[2, 0][0][:].rearrange("p j (t c i) -> p t c j i", t=2, i=PACK),
+        )
 
         z_rows = keep.tile([P, BLOCKS * H], BF16, name="z_rows", align_bytes=64)
         z_view = z_rows[:].rearrange("v (b u p e) -> v b u p e", b=BLOCKS, u=2, e=2)
@@ -255,8 +252,8 @@ def tile_picked_lapl_silu_p_kernel(
             for b in range(b0, b1):
                 terms[name, t, b] = tile[:, (b - b0) * P : (b - b0 + 1) * P]
 
-        def centres(t, b0, b1):
-            own = keep.tile([P, (b1 - b0) * P], F32, name=f"own{t}_{b0}", tag=f"own{t}")
+        def centres(t, b0, b1, tag=None):
+            own = keep.tile([P, (b1 - b0) * P], F32, name=f"own{t}_{b0}", tag=tag or f"own{t}", align_bytes=64)
             columns = slice(b0 * P // PER_COLUMN, b1 * P // PER_COLUMN)
             nc.scalar.activation(own[:], h[t][:].indirect(cen_sb[:, columns]), COPY)
             keep_terms("own", t, b0, b1, own)
@@ -333,12 +330,12 @@ def tile_picked_lapl_silu_p_kernel(
         on_scalar, on_vector = nc.scalar.copy, nc.vector.tensor_copy
         centres(0, 0, 4)
         first0 = tile_for([P, V], F32, "first0")
-        neighbours(0, 0, 0, 2, first0[:, 0 : V // 2], "first")
-        neighbours(0, 0, 2, 4, first0[:, V // 2 : V])
-        rounded_tile("w1_b", [(2, 1), (3, 1)])
-        round_w1("w1_b", 2, 4, 1, nc.vector.tensor_copy)
-        quantize_w1("w1_a")
-        quantize_w1("w1_b")
+        neighbours(0, 0, 0, 4, first0)
+        quantize_w1("w1_23", 0, 1)
+        round_w1("w1_23", 2, 3, 1, nc.vector.tensor_copy)
+        round_w1("w1_23", 3, 4, 1, nc.vector.tensor_copy)
+        quantize_w1("w1_23", 1, 2)
+        quantize_w1("w1_23", 2, 4)
         first_layer(2, 0, 512, 4)
         first_layer(2, 512, 1024, 5)
         first_layer(3, 0, 512, 0)
@@ -347,10 +344,10 @@ def tile_picked_lapl_silu_p_kernel(
         neighbours(1, 0, 0, 4, later[:, 0:V])
         neighbours(0, 1, 0, 4, later[:, V : 2 * V])
         neighbours(1, 1, 0, 4, later[:, 2 * V : 3 * V])
-        add_terms(0, 0, 4, 6, (0, "own", 1))
+        add_terms(0, 0, 4, 4, (0, "own", 1))
         centres(1, 0, 4)
-        centres(2, 0, 4)
-        add_terms(1, 0, 4, 7)
+        centres(2, 0, 4, "w1_23_codes2")
+        add_terms(1, 0, 4, 5)
         centres(3, 0, 2)
         round_z(0, 0, 0, 4, on_scalar)
         round_z(1, 0, 0, 4, on_scalar)
@@ -366,22 +363,22 @@ def tile_picked_lapl_silu_p_kernel(
         for d in range(NEIGHBOURS):
             late = keep.tile([P, V // 2], F32, name=f"late{d}", tag=f"early_weights{d}")
             neighbours(d, 2, 2, 4, late)
-        add_terms(2, 2, 4, 4)
+        add_terms(2, 2, 4, 6)
         round_z(2, 2, 2, 4, on_scalar)
-        turn_back(0, 2, (5, 0), on_scalar)
+        turn_back(0, 2, (7, 0), on_scalar)
         neighbours(0, 3, 2, 3)
         neighbours(1, 3, 2, 3)
         add_terms(3, 2, 3, 1)
         neighbours(0, 3, 3, 4)
         neighbours(1, 3, 3, 4)
-        add_terms(3, 3, 4, 6)
+        add_terms(3, 3, 4, 4)
         round_z(3, 2, 2, 3, on_scalar)
         round_z(3, 3, 3, 4, on_scalar)
         quantize_z(0, 2)
-        turn_back(2, 3, (7,), on_scalar)
+        turn_back(2, 3, (5,), on_scalar)
         turn_back(3, 4, (2,), on_scalar)
-        second_layer(0, 2, 6, on_vector, nc.sync)
+        second_layer(0, 2, 4, on_vector, nc.sync)
         quantize_z(2, 3)
         quantize_z(3, 4)
         second_layer(2, 3, 3, on_vector, nc.sync)
-        second_layer(3, 4, 4, on_scalar, nc.scalar)
+        second_layer(3, 4, 6, on_scalar, nc.scalar)

@@ -220,7 +220,7 @@ def tile_picked_lapl_silu_p_kernel(
         w2_codes = tile_for([P, 2 * N], U8, "w2_codes")
         nc.sync.dma_start(w2_codes[:].bitcast(I32), w2_words[0].bitcast(I32))
         w2_plane = tile_for([P, N], U8, "w2_plane")
-        nc.vector.memset(w2_plane[:].bitcast(I32), 0)
+        nc.gpsimd.memset(w2_plane[:].bitcast(I32), 0)
         for q in range(QUADRANTS):
             nc.sync.dma_start(
                 w2_plane[32 * q : 32 * q + 4, :].bitcast(I32),
@@ -236,10 +236,9 @@ def tile_picked_lapl_silu_p_kernel(
         quantize_w1("w1_1")
         first_layer(1, 0, 512, 2)
         first_layer(1, 512, 1024, 3)
-        nc.vector.tensor_copy(
-            w1_grouped["w1_23"][0][:].rearrange("p (t g c i j) -> p g t c j i", t=2, g=PASSES, i=PACK, j=PACK)[:, 0],
-            w1_raw[2, 0][0][:].rearrange("p j (t c i) -> p t c j i", t=2, i=PACK),
-        )
+        round_w1("w1_23", 2, 3, 0, nc.vector.tensor_copy)
+        round_w1("w1_23", 3, 4, 0, nc.vector.tensor_copy)
+        quantize_w1("w1_23", 0, 1)
 
         z_rows = keep.tile([P, BLOCKS * H], BF16, name="z_rows", align_bytes=64)
         z_view = z_rows[:].rearrange("v (b u p e) -> v b u p e", b=BLOCKS, u=2, e=2)
@@ -331,7 +330,6 @@ def tile_picked_lapl_silu_p_kernel(
         centres(0, 0, 4)
         first0 = tile_for([P, V], F32, "first0")
         neighbours(0, 0, 0, 4, first0)
-        quantize_w1("w1_23", 0, 1)
         round_w1("w1_23", 2, 3, 1, nc.vector.tensor_copy)
         round_w1("w1_23", 3, 4, 1, nc.vector.tensor_copy)
         quantize_w1("w1_23", 1, 2)

@@ -182,13 +182,17 @@ def tile_picked_lapl_silu_p_kernel(
 
         h = {}
 
-        def first_layer(t, c0, c1, number):
+        h_acc = {}
+
+        def first_layer(t, c0, c1, number, passes=(0, 1)):
             if t not in h:
                 h[t] = tile_for([P, S], F32, f"h{t}")
-            acc = bank(number, [P, c1 - c0], "h_acc")
+            if 0 in passes:
+                h_acc[t, c0] = bank(number, [P, c1 - c0], "h_acc")
+            acc = h_acc[t, c0]
             runs = [
                 (g, max(c0, e0), min(c1, e1), e0, words)
-                for g in range(PASSES)
+                for g in passes
                 for e0, e1, words in picked[g]
                 if e0 < c1 and e1 > c0
             ]
@@ -200,10 +204,11 @@ def tile_picked_lapl_silu_p_kernel(
                     lhsT_scale=plane,
                     rhs=words[:, a - e0 : b - e0].bitcast(FP8X4),
                     rhs_scale=picked_plane[4 * g : P, a:b],
-                    start=(i == 0),
-                    stop=(i == len(runs) - 1),
+                    start=(g == 0),
+                    stop=(g == 1 and i == len(runs) - 1),
                 )
-            nc.scalar.activation(h[t][:, c0:c1], acc[:], SILU)
+            if 1 in passes:
+                nc.scalar.activation(h[t][:, c0:c1], acc[:], SILU)
 
         rounded_tile("w1_00", [(0, 0)])
         rounded_tile("w1_01", [(0, 1)])
@@ -229,8 +234,9 @@ def tile_picked_lapl_silu_p_kernel(
         pick(1, 512, 768, (512, 768))
         quantize_w1("w1_01")
         pick(1, 768, 1024, (768, 1024))
-        first_layer(0, 0, 512, 0)
-        first_layer(0, 512, 768, 1)
+        for g in range(PASSES):
+            for c0, number in ((0, 0), (256, 6), (512, 1)):
+                first_layer(0, c0, c0 + 256, number, (g,))
         first_layer(0, 768, 1024, 7)
         round_w1("w1_1", 1, 2, 1, nc.vector.tensor_copy)
         quantize_w1("w1_1")

@@ -348,10 +348,10 @@ def tile_picked_lapl_silu_p_kernel(
         neighbours(1, 0, 0, 4, later[:, 0:V])
         neighbours(0, 1, 0, 4, later[:, V : 2 * V])
         neighbours(1, 1, 0, 4, later[:, 2 * V : 3 * V])
-        add_terms(0, 0, 4, 4, (0, "own", 1))
+        add_terms(0, 0, 4, 6, (1, "own", 0))
         centres(1, 0, 4)
         centres(2, 0, 4, "w1_23_codes2")
-        add_terms(1, 0, 4, 5)
+        add_terms(1, 0, 4, 7)
         centres(3, 0, 2)
         round_z(0, 0, 0, 4, on_scalar)
         round_z(1, 0, 0, 4, on_scalar)
@@ -367,22 +367,22 @@ def tile_picked_lapl_silu_p_kernel(
         for d in range(NEIGHBOURS):
             late = keep.tile([P, V // 2], F32, name=f"late{d}", tag=f"early_weights{d}")
             neighbours(d, 2, 2, 4, late)
-        add_terms(2, 2, 4, 6)
+        add_terms(2, 2, 4, 4)
         round_z(2, 2, 2, 4, on_scalar)
-        turn_back(0, 2, (7, 0), on_scalar)
+        turn_back(0, 2, (5, 0), on_scalar)
         neighbours(0, 3, 2, 3)
         neighbours(1, 3, 2, 3)
         add_terms(3, 2, 3, 1)
         neighbours(0, 3, 3, 4)
         neighbours(1, 3, 3, 4)
-        add_terms(3, 3, 4, 4)
+        add_terms(3, 3, 4, 6)
         round_z(3, 2, 2, 3, on_scalar)
         round_z(3, 3, 3, 4, on_scalar)
         quantize_z(0, 2)
-        turn_back(2, 3, (5,), on_scalar)
+        turn_back(2, 3, (7,), on_scalar)
         turn_back(3, 4, (2,), on_scalar)
-        second_layer(0, 2, 4, on_vector, nc.sync)
+        second_layer(0, 2, 6, on_vector, nc.sync)
         quantize_z(2, 3)
         quantize_z(3, 4)
         second_layer(2, 3, 3, on_vector, nc.sync)
-        second_layer(3, 4, 6, on_scalar, nc.scalar)
+        second_layer(3, 4, 4, on_scalar, nc.scalar)

@@ -102,9 +102,8 @@ def tile_picked_lapl_silu_p_kernel(
         for g in range(PASSES):
             rows = x_scales[g].bitcast(I32).rearrange("(q r) n -> r q n", r=4)
             nc.sync.dma_start(x_rows[16 * g : 16 * (g + 1), :].bitcast(I32), rows)
-        nc.sync.dma_start(
-            gate_rows[0 : NEIGHBOURS * BLOCKS, :], gate[:, 0, :].rearrange("d (b k) -> d b k", k=P)
-        )
+        pieces = gate.rearrange("d p (b k) -> (d p b) k", k=P)
+        nc.sync.dma_start(gate_rows[0 : NEIGHBOURS * BLOCKS, :], pieces[0 :: P + 1, :])
         load_x(0)
         pos1_sb = load_list("pos1_sb", pos1, V)
         cen_sb = load_list("cen_sb", cen, V)
@@ -120,7 +119,7 @@ def tile_picked_lapl_silu_p_kernel(
 
         picked_rows = keep.tile([P, S], U8, name="picked_rows", align_bytes=64)
         nc.vector.tensor_copy(picked_rows[:], x_rows[:].indirect(offs_sb[:]))
-        for q in range(QUADRANTS):
+        for q in (0, 2, 1, 3):
             nc.sync.dma_start(
                 picked_plane[32 * q : 32 * q + 8, :].bitcast(I32), picked_rows[q:32:4, :].bitcast(I32)
             )

@@ -54,7 +54,8 @@ def tile_picked_lapl_silu_p_kernel(
             "w2_codes": 14208,
             "w2_plane": 14464,
             "w1_raw2_0": 14592,
-            "first0": 14592,
+            "w1_raw3_0": 16640,
+            "first0": 16640,
             "w1_raw0_0": 25408,
             "picked1_512": 25408,
             "w1_raw0_1": 27456,
@@ -219,8 +220,9 @@ def tile_picked_lapl_silu_p_kernel(
         pick(0, 0, S, (0, S))
         pick(1, 0, 512, (0, 512))
         quantize_w1("w1_00")
-        for g in range(PASSES):
-            load_w1(W1_LOADS[2], g)
+        load_w1((2, 3), 0)
+        load_w1((3, 4), 0)
+        load_w1((2, 4), 1)
         w2_codes = tile_for([P, 2 * N], U8, "w2_codes")
         nc.sync.dma_start(w2_codes[:].bitcast(I32), w2_words[0].bitcast(I32))
         w2_plane = tile_for([P, N], U8, "w2_plane")
@@ -242,8 +244,8 @@ def tile_picked_lapl_silu_p_kernel(
         first_layer(1, 0, 512, 2)
         first_layer(1, 512, 1024, 3)
         round_w1("w1_23", 2, 3, 0, nc.vector.tensor_copy)
-        round_w1("w1_23", 3, 4, 0, nc.vector.tensor_copy)
         quantize_w1("w1_23", 0, 1)
+        round_w1("w1_23", 3, 4, 0, nc.vector.tensor_copy)
 
         z_rows = keep.tile([P, BLOCKS * H], BF16, name="z_rows", align_bytes=64)
         z_view = z_rows[:].rearrange("v (b u p e) -> v b u p e", b=BLOCKS, u=2, e=2)

from contextlib import ExitStack

import concourse.mybir as mybir
from concourse.masks import make_identity

K, T, S, V, H, N = 1024, 2048, 1024, 512, 512, 128
FLOPS = 2 * K * H * S + 2 * H * N * V

F32 = mybir.dt.float32
BF16 = mybir.dt.bfloat16
I32 = mybir.dt.int32
U32 = mybir.dt.uint32
U16 = mybir.dt.uint16
U8 = mybir.dt.uint8
FP8X4 = mybir.dt.float8_e4m3fn_x4
FP4X4 = mybir.dt.float4_e2m1fn_x4
COPY = mybir.ActivationFunctionType.Copy
SILU = mybir.ActivationFunctionType.Silu
MULT = mybir.AluOpType.mult

P = 128
PACK = 4
QUADRANTS = 4
PER_COLUMN = 16
PASSES = K // (P * PACK)
BANK = 512
BLOCKS = V // P
NEIGHBOURS = 2

W1_LOADS = ((0, 1), (1, 2), (2, 4))


def tile_picked_lapl_silu_p_kernel(
    tc, x_words, x_scales, w1, w2_words, w2_scales, gate, offs, cen, pos1, pos2, out
):
    nc = tc.nc
    with ExitStack() as ctx:
        lists = ctx.enter_context(tc.tile_pool(name="lists", bufs=1))
        keep = ctx.enter_context(tc.tile_pool(name="keep", bufs=1))
        psum = ctx.enter_context(tc.psum_pool(name="psum", bufs=1))

        def bank(number, shape, name):
            return psum.tile(shape, F32, name=name, tag=f"bank{number}")

        placed = ctx.enter_context(tc.tile_pool(name="placed", bufs=1))
        offsets_of = {
            "w1_raw1_1": 0,
            "x_rows": 1984,
            "w1_raw1_0": 3968,
            "h0": 3968,
            "w1_raw2_1": 8064,
            "later": 8064,
            "x_table0": 12096,
            "w2_codes": 14208,
            "w2_plane": 14464,
            "w1_raw2_0": 14592,
            "w1_raw3_0": 16640,
            "first0": 16640,
            "w1_raw0_0": 25408,
            "picked1_512": 25408,
            "w1_raw0_1": 27456,
            "picked1_768": 27456,
        }

        def tile_for(shape, dtype, name):
            if name in offsets_of:
                return placed.tile(shape, dtype, name=name, offset=offsets_of[name], align_bytes=64)
            return keep.tile(shape, dtype, name=name, tag=name, align_bytes=64)

        gate_rows = keep.tile([P, P], F32, name="gate_rows")
        nc.gpsimd.memset(gate_rows[:], 0.0)
        warm_in = keep.tile([P, 1], F32, name="warm_in")
        warm_out = keep.tile([P, 1], F32, name="warm_out")
        nc.gpsimd.memset(warm_in[:], 0.0)
        nc.scalar.activation(warm_out[:], warm_in[:], SILU)
        x_rows = tile_for([P, T], U8, "x_rows")
        nc.gpsimd.memset(x_rows[32:64, :].bitcast(I32), 0)
        nc.gpsimd.memset(x_rows[64:P, :].bitcast(I32), 0)

        def load_list(name, source, entries):
            tile = lists.tile([P, entries // PER_COLUMN], U16, name=name)
            nc.sync.dma_start(tile[:], source)
            return tile

        w1_raw = {}

        def load_w1(tiles, g):
            t0, t1 = tiles
            raw = tile_for([P, PACK, (t1 - t0) * P], F32, f"w1_raw{t0}_{g}")
            rows = w1[g * P * PACK : (g + 1) * P * PACK, t0 * P : t1 * P]
            nc.sync.dma_start(raw[:], rows.rearrange("(p j) c -> p j c", j=PACK))
            for t in range(t0, t1):
                w1_raw[t, g] = (raw, t0)

        x_table = []

        def load_x(g):
            table = tile_for([P, T], I32, f"x_table{g}")
            nc.sync.dma_start(table[:], x_words[g].rearrange("p n t -> p (n t)").bitcast(I32))
            x_table.append(table)

        offs_sb = load_list("offs_sb", offs, S)
        for g in range(PASSES):
            rows = x_scales[g].bitcast(I32).rearrange("(q r) n -> r q n", r=4)
            nc.sync.dma_start(x_rows[16 * g : 16 * (g + 1), :].bitcast(I32), rows)
        pieces = gate.rearrange("d p (b k) -> (d p b) k", k=P)
        nc.sync.dma_start(gate_rows[0 : NEIGHBOURS * BLOCKS, :], pieces[0 :: P + 1, :])
        load_x(0)
        pos1_sb = load_list("pos1_sb", pos1, V)
        cen_sb = load_list("cen_sb", cen, V)
        pos2_sb = load_list("pos2_sb", pos2, V)
        load_x(1)
        for g in range(PASSES):
            load_w1(W1_LOADS[0], g)

        identity = keep.tile([P, P], F32, name="identity")
        make_identity(nc, identity[:])
        picked_plane = keep.tile([P, S], U8, name="picked_plane", align_bytes=64)
        nc.gpsimd.memset(picked_plane[:].bitcast(I32), 0)

        picked_rows = keep.tile([P, S], U8, name="picked_rows", align_bytes=64)
        nc.vector.tensor_copy(picked_rows[:], x_rows[:].indirect(offs_sb[:]))
        for q in (0, 2, 1, 3):
            nc.sync.dma_start(
                picked_plane[32 * q : 32 * q + 8, :].bitcast(I32), picked_rows[q:32:4, :].bitcast(I32)
            )
        for g in range(PASSES):
            load_w1(W1_LOADS[1], g)

        gate_turned = bank(2, [P, P], "gate_turned")
        nc.tensor.transpose(gate_turned[:], gate_rows[:], identity[:])
        gate_cols = keep.tile([P, NEIGHBOURS * BLOCKS], F32, name="gate_cols", tag="w1_00", align_bytes=64)
        nc.scalar.copy(gate_cols[:], gate_turned[:, 0 : NEIGHBOURS * BLOCKS])
        edge_weights = {}
        for d in range(NEIGHBOURS):
            spread = bank(3 + d, [P, BLOCKS, P], "spread")
            for b in range(BLOCKS):
                column = gate_cols[:, BLOCKS * d + b : BLOCKS * d + b + 1]
                nc.tensor.transpose(spread[:, b, :], column.to_broadcast([P, P]), identity[:])
            signed = keep.tile([P, V], F32, name=f"edge_weights{d}")
            nc.scalar.activation(signed[:], spread[:].rearrange("p b k -> p (b k)"), COPY, scale=-1.0)
            edge_weights[d, "all"] = signed
            early = keep.tile([P, V // 2], F32, name=f"early_weights{d}", tag=f"early_weights{d}")
            nc.scalar.activation(early[:], spread[:, 0:2, :].rearrange("p b k -> p (b k)"), COPY, scale=-1.0)
            edge_weights[d, "early"] = early

        picked = {0: [], 1: []}

        def pick(g, e0, e1, borders):
            words = tile_for([P, e1 - e0], U32, f"picked{g}_{e0}")
            for a, b in zip(borders, borders[1:]):
                offsets = offs_sb[:, a // PER_COLUMN : b // PER_COLUMN]
                nc.vector.tensor_copy(words[:, a - e0 : b - e0], x_table[g][:].bitcast(U32).indirect(offsets))
            picked[g].append((e0, e1, words))

        w1_grouped = {}
        w1_mx = {}

        def rounded_tile(name, parts):
            tile = tile_for([P, len(parts) * P * PACK], BF16, name)
            w1_grouped[name] = (tile, parts)

        def round_w1(name, t0, t1, g, copy):
            tile, parts = w1_grouped[name]
            first = parts.index((t0, g))
            raw, base = w1_raw[t0, g]
            copy(
                tile[:, first * P * PACK : (first + t1 - t0) * P * PACK].rearrange("p (c i j) -> p c j i", i=PACK, j=PACK),
                raw[:, :, (t0 - base) * P : (t1 - base) * P].rearrange("p j (c i) -> p c j i", i=PACK),
            )

        def quantize_w1(name, first=0, end=None):
            tile, parts = w1_grouped[name]
            parts = parts[first:end]
            width = len(parts) * P
            codes = tile_for([P, width], U32, f"{name}_codes{first}")
            plane = keep.tile([P, width], U8, name=f"{name}_plane{first}", align_bytes=64)
            source = tile[:, first * P * PACK : first * P * PACK + width * PACK]
            nc.vector.quantize_mx(out=codes[:].bitcast(FP8X4), scales=plane[:], in_=source)
            for i, part in enumerate(parts):
                w1_mx[part] = (codes[:, i * P : (i + 1) * P], plane[:, i * P : (i + 1) * P])

        h = {}

        h_acc = {}

        def first_layer(t, c0, c1, number, passes=(0, 1)):
            if t not in h:
                h[t] = tile_for([P, S], F32, f"h{t}")
            if 0 in passes:
                h_acc[t, c0] = bank(number, [P, c1 - c0], "h_acc")
            acc = h_acc[t, c0]
            runs = [
                (g, max(c0, e0), min(c1, e1), e0, words)
                for g in passes
                for e0, e1, words in picked[g]
                if e0 < c1 and e1 > c0
            ]
            for i, (g, a, b, e0, words) in enumerate(runs):
                codes, plane = w1_mx[t, g]
                nc.tensor.matmul_mx(
                    out=acc[:, a - c0 : b - c0],
                    lhsT=codes.bitcast(FP8X4),
                    lhsT_scale=plane,
                    rhs=words[:, a - e0 : b - e0].bitcast(FP8X4),
                    rhs_scale=picked_plane[4 * g : P, a:b],
                    start=(g == 0),
                    stop=(g == 1 and i == len(runs) - 1),
                )
            if 1 in passes:
                nc.scalar.activation(h[t][:, c0:c1], acc[:], SILU)

        rounded_tile("w1_00", [(0, 0)])
        rounded_tile("w1_01", [(0, 1)])
        rounded_tile("w1_1", [(1, 0), (1, 1)])
        rounded_tile("w1_23", [(2, 0), (2, 1), (3, 0), (3, 1)])
        round_w1("w1_00", 0, 1, 0, nc.scalar.copy)
        round_w1("w1_01", 0, 1, 1, nc.scalar.copy)
        round_w1("w1_1", 1, 2, 0, nc.scalar.copy)
        pick(0, 0, S, (0, S))
        pick(1, 0, 512, (0, 512))
        quantize_w1("w1_00")
        load_w1((2, 3), 0)
        load_w1((3, 4), 0)
        load_w1((2, 4), 1)
        w2_codes = tile_for([P, 2 * N], U8, "w2_codes")
        nc.sync.dma_start(w2_codes[:].bitcast(I32), w2_words[0].bitcast(I32))
        w2_plane = tile_for([P, N], U8, "w2_plane")
        nc.gpsimd.memset(w2_plane[:].bitcast(I32), 0)
        for q in range(QUADRANTS):
            nc.sync.dma_start(
                w2_plane[32 * q : 32 * q + 4, :].bitcast(I32),
                w2_scales[0, 4 * q : 4 * q + 4, :].bitcast(I32),
            )
        pick(1, 512, 768, (512, 768))
        quantize_w1("w1_01")
        pick(1, 768, 1024, (768, 1024))
        for g in range(PASSES):
            for c0, number in ((0, 0), (256, 6), (512, 1)):
                first_layer(0, c0, c0 + 256, number, (g,))
        first_layer(0, 768, 1024, 7)
        round_w1("w1_1", 1, 2, 1, nc.vector.tensor_copy)
        quantize_w1("w1_1")
        first_layer(1, 0, 512, 2)
        first_layer(1, 512, 1024, 3)
        round_w1("w1_23", 2, 3, 0, nc.vector.tensor_copy)
        quantize_w1("w1_23", 0, 1)
        round_w1("w1_23", 3, 4, 0, nc.vector.tensor_copy)

        z_rows = keep.tile([P, BLOCKS * H], BF16, name="z_rows", align_bytes=64)
        z_view = z_rows[:].rearrange("v (b u p e) -> v b u p e", b=BLOCKS, u=2, e=2)
        z_pairs = z_rows[:].bitcast(F32)

        terms = {}
        sums = {}

        def keep_terms(name, t, b0, b1, tile):
            for b in range(b0, b1):
                terms[name, t, b] = tile[:, (b - b0) * P : (b - b0 + 1) * P]

        def centres(t, b0, b1, tag=None):
            own = keep.tile([P, (b1 - b0) * P], F32, name=f"own{t}_{b0}", tag=tag or f"own{t}", align_bytes=64)
            columns = slice(b0 * P // PER_COLUMN, b1 * P // PER_COLUMN)
            nc.scalar.activation(own[:], h[t][:].indirect(cen_sb[:, columns]), COPY)
            keep_terms("own", t, b0, b1, own)

        def neighbours(d, t, b0, b1, term=None, weights="all"):
            if term is None:
                term = keep.tile([P, (b1 - b0) * P], F32, name=f"neighbour{d}_{t}_{b0}")
            columns = slice(b0 * P // PER_COLUMN, b1 * P // PER_COLUMN)
            offsets = (pos1_sb, pos2_sb)[d][:, columns]
            nc.vector.tensor_tensor(term[:], h[t][:].indirect(offsets), edge_weights[d, weights][:, b0 * P : b1 * P], MULT)
            keep_terms(d, t, b0, b1, term)

        def add_terms(t, b0, b1, number, names=("own", 0, 1)):
            acc = bank(number, [P, b1 - b0, P], "z_acc")
            for i, name in enumerate(names):
                for b in range(b0, b1):
                    nc.tensor.matmul(
                        acc[:, b - b0, :],
                        lhsT=terms[name, t, b],
                        rhs=identity[:],
                        is_transpose=True,
                        start=(i == 0 and b == b0),
                        stop=(i == 2 and b == b1 - 1),
                    )
            sums[t, b0] = acc

        def round_z(t, start, b0, b1, copy):
            copy(
                z_view[:, b0:b1, :, 32 * t : 32 * (t + 1), :],
                sums[t, start][:, b0 - start : b1 - start, :].rearrange("v b (p u e) -> v b u p e", u=2, e=2),
            )

        z_grouped = {}

        def turn_back(b0, b1, numbers, copy):
            grouped = keep.tile([P, (b1 - b0) * P * PACK], BF16, name=f"z_grouped{b0}", align_bytes=64)
            for b in range(b0, b1):
                turned = bank(numbers[b - b0], [P, 2, P], "turned")
                for u in range(2):
                    c0 = (2 * b + u) * P
                    nc.tensor.transpose(turned[:, u, :], z_pairs[:, c0 : c0 + P], identity[:])
                copy(
                    grouped[:, (b - b0) * P * PACK : (b - b0 + 1) * P * PACK].bitcast(F32).rearrange("p (v u) -> p v u", u=2),
                    turned[:].rearrange("p u v -> p v u"),
                )
            z_grouped[b0] = grouped

        z_mx = {}

        def quantize_z(b0, b1):
            width = (b1 - b0) * P
            codes = keep.tile([P, width], U32, name=f"z_codes{b0}", align_bytes=64)
            plane = keep.tile([P, width], U8, name=f"z_plane{b0}", align_bytes=64)
            nc.vector.quantize_mx(out=codes[:].bitcast(FP8X4), scales=plane[:], in_=z_grouped[b0][:])
            z_mx[b0] = (codes, plane)

        def second_layer(b0, b1, number, copy, queue):
            width = (b1 - b0) * P
            codes, plane = z_mx[b0]
            acc = bank(number, [P, width], "out_acc")
            nc.tensor.matmul_mx(
                out=acc[:],
                lhsT=w2_codes[:].bitcast(FP4X4),
                lhsT_scale=w2_plane[:],
                rhs=codes[:].bitcast(FP8X4),
                rhs_scale=plane[:],
                start=True,
                stop=True,
            )
            result = keep.tile([P, width], F32, name=f"result{b0}")
            copy(result[:], acc[:])
            queue.dma_start(out[:, b0 * P : b1 * P], result[:])

        on_scalar, on_vector = nc.scalar.copy, nc.vector.tensor_copy
        centres(0, 0, 4)
        first0 = tile_for([P, V], F32, "first0")
        neighbours(0, 0, 0, 4, first0)
        round_w1("w1_23", 2, 3, 1, nc.vector.tensor_copy)
        round_w1("w1_23", 3, 4, 1, nc.vector.tensor_copy)
        quantize_w1("w1_23", 1, 2)
        quantize_w1("w1_23", 2, 4)
        first_layer(2, 0, 512, 4)
        first_layer(2, 512, 1024, 5)
        first_layer(3, 0, 512, 0)
        first_layer(3, 512, 1024, 1)
        later = tile_for([P, 3 * V], F32, "later")
        neighbours(1, 0, 0, 4, later[:, 0:V])
        neighbours(0, 1, 0, 4, later[:, V : 2 * V])
        neighbours(1, 1, 0, 4, later[:, 2 * V : 3 * V])
        add_terms(0, 0, 4, 6, (1, "own", 0))
        centres(1, 0, 4)
        centres(2, 0, 4, "w1_23_codes2")
        add_terms(1, 0, 4, 7)
        centres(3, 0, 2)
        round_z(0, 0, 0, 4, on_scalar)
        round_z(1, 0, 0, 4, on_scalar)
        neighbours(0, 2, 0, 2)
        neighbours(1, 2, 0, 2)
        add_terms(2, 0, 2, 2, (0, "own", 1))
        neighbours(0, 3, 0, 2, None, "early")
        neighbours(1, 3, 0, 2, None, "early")
        add_terms(3, 0, 2, 3)
        round_z(2, 0, 0, 2, on_scalar)
        round_z(3, 0, 0, 2, on_scalar)
        centres(3, 2, 4)
        for d in range(NEIGHBOURS):
            late = keep.tile([P, V // 2], F32, name=f"late{d}", tag=f"early_weights{d}")
            neighbours(d, 2, 2, 4, late)
        add_terms(2, 2, 4, 4)
        round_z(2, 2, 2, 4, on_scalar)
        turn_back(0, 2, (5, 0), on_scalar)
        neighbours(0, 3, 2, 3)
        neighbours(1, 3, 2, 3)
        add_terms(3, 2, 3, 1)
        neighbours(0, 3, 3, 4)
        neighbours(1, 3, 3, 4)
        add_terms(3, 3, 4, 6)
        round_z(3, 2, 2, 3, on_scalar)
        round_z(3, 3, 3, 4, on_scalar)
        quantize_z(0, 2)
        turn_back(2, 3, (7,), on_scalar)
        turn_back(3, 4, (2,), on_scalar)
        second_layer(0, 2, 6, on_vector, nc.sync)
        quantize_z(2, 3)
        quantize_z(3, 4)
        second_layer(2, 3, 3, on_vector, nc.sync)
        second_layer(3, 4, 4, on_scalar, nc.scalar)
